import numpy as np
import ml_dtypes


def mxq(x, axis, fmt="e4m3"):
    dtype, down = {"e4m3": (ml_dtypes.float8_e4m3fn, 7), "e5m2": (ml_dtypes.float8_e5m2, 14)}[fmt]
    v = np.moveaxis(np.asarray(x, np.float32).astype(ml_dtypes.bfloat16).astype(np.float64), axis, -1)
    blocks = v.reshape(v.shape[:-1] + (-1, 32))
    amax = np.abs(blocks).max(-1, keepdims=True)
    byte = np.maximum(np.where(amax > 0, np.frexp(amax)[1] - 1 + 127, 0) - down, 1)
    scale = np.exp2(byte - 127.0)
    codes = (blocks / scale).astype(np.float32).astype(dtype).astype(np.float64)
    return np.moveaxis((codes * scale).reshape(v.shape), -1, axis)


WIDE = False


def mx_kscale(k):
    if not WIDE:
        return np.ones(k)
    levels = np.array([10, -10, 5, -5, 0])
    if k % 512:
        return np.exp2(np.random.permutation(np.resize(levels, k // 32))).repeat(32)
    a = np.empty((k // 512, 16))
    for p in range(k // 512):
        a[p, :8] = np.random.permutation(np.resize(levels, 8))
        for g in range(8):
            far = levels[np.abs(levels - a[p, g]) >= 10]
            a[p, g + 8] = far[np.random.randint(len(far))]
    return np.exp2(a.ravel()).repeat(32)


def f64(x):
    return np.asarray(x).astype(np.float64)


def striped(idx):
    return np.tile(np.asarray(idx).reshape(-1, 16).T, (8, 1)).astype(np.uint16)


def unstriped(offs):
    return offs[:16].T.reshape(-1).astype(np.int64)


G, K, T, D, M = 512, 4, 4096, 512, 256


def setup_inputs():
    n = np.random.standard_normal
    s = mx_kscale(D)[:, None]
    grid = lambda x: np.round(x * 32) / 32
    x = grid(n((D, T))) * s
    idx = np.random.randint(0, T, (G, K))
    part = np.random.randint(1, 128 // K, (G, K)) / 64.0
    return {
        "xT": x.astype(np.float32),
        "w": (n((D, M)) / np.sqrt(D) / s).astype(np.float32),
        "part": np.tile(part.reshape(-1), (128, 1)).astype(np.float32),
        "offs": striped(idx.reshape(-1)),
    }


def reference(xT, w, part, offs):
    x = f64(xT)[:, unstriped(offs)]
    y = mxq(f64(w), 0, "e4m3").T @ mxq((x * f64(part)[:1]).reshape(D, G, K).sum(-1), 0, "e4m3")
    return y

@@ -1,0 +1,167 @@
+from contextlib import ExitStack
+
+import concourse.mybir as mybir
+from concourse.masks import make_identity
+
+F32 = mybir.dt.float32
+BF16 = mybir.dt.bfloat16
+U32 = mybir.dt.uint32
+U16 = mybir.dt.uint16
+U8 = mybir.dt.uint8
+FP8X4 = mybir.dt.float8_e4m3fn_x4
+MULT = mybir.AluOpType.mult
+ADD = mybir.AluOpType.add
+
+P = 128
+T = 4096
+D = 512
+M = 256
+G = 512
+K = 4
+E = G * K
+PACK = 4
+FLOPS = 2 * D * M * G
+
+PIECES = ((1024, 1024), (1024, 1024), (1024, 512, 512), (512, 512, 512, 512))
+
+
+def tile_attend_grid_kernel(tc, xT, w, part, offs, out):
+    nc = tc.nc
+    x_planes = xT.rearrange("(p t) c -> p t c", t=PACK)
+    with ExitStack() as ctx:
+        held = ctx.enter_context(tc.tile_pool(name="held", bufs=1))
+        ring = ctx.enter_context(tc.tile_pool(name="ring", bufs=4))
+        wide = ctx.enter_context(tc.tile_pool(name="wide", bufs=3))
+        psum = ctx.enter_context(tc.psum_pool(name="psum", bufs=1))
+
+        offsets = held.tile([P, E // 16], U16, name="offsets")
+        nc.sync.dma_start(offsets[:], offs)
+        part_col = held.tile([P, E // P], F32, name="part_col")
+        nc.scalar.dma_start(part_col[:], part[0:1, :].rearrange("o (q i) -> (o q) i", i=E // P))
+        planes = []
+        for t in range(PACK):
+            plane = held.tile([P, T], F32, name=f"plane{t}")
+            for h in range(2):
+                cols = slice(h * T // 2, (h + 1) * T // 2)
+                nc.sync.dma_start(plane[:, cols], x_planes[:, t, cols])
+            planes.append(plane)
+        w_raw = held.tile([P, PACK, M], F32, name="w_raw")
+        nc.sync.dma_start(w_raw[:], w.rearrange("(p t) m -> p t m", t=PACK))
+
+        ident = held.tile([P, P], F32, name="ident")
+        make_identity(nc, ident[:])
+
+        part_rep = held.tile([P, E], F32, name="part_rep")
+        part_view = part_rep[:].rearrange("p (q i) -> p q i", i=E // P)
+        for b in range(4):
+            bank = psum.tile([P, 4, P], F32, name=f"part_bank{b}", tag=f"back{b}")
+            for i in range(4):
+                col = part_col[:, 4 * b + i : 4 * b + i + 1]
+                nc.tensor.transpose(bank[:, i, :], col.to_broadcast([P, P]), ident[:])
+            src = bank[:].rearrange("p i q -> p q i")
+            dst = part_view[:, :, 4 * b : 4 * b + 4]
+            if b % 2 == 0:
+                nc.vector.tensor_copy(dst, src)
+            else:
+                nc.scalar.copy(dst, src)
+
+        sums = [psum.tile([P, PACK, P], F32, name=f"sums{k}", tag=f"fore{k}") for k in range(4)]
+        backs = [psum.tile([P, PACK, P], F32, name=f"backs{k}", tag=f"back{k}") for k in range(4)]
+
+        w_grouped = held.tile([P, M, PACK], BF16, name="w_grouped", align_bytes=64)
+        w_codes = held.tile([P, M], U32, name="w_codes", align_bytes=64)
+        w_scales = held.tile([P, M], U8, name="w_scales", align_bytes=64)
+        last_e = held.tile([P, PACK, P], F32, name="last_e")
+        nc.gpsimd.memset(last_e[:, 3, :], 0.0)
+        fourth = held.tile([P, P, PACK], BF16, name="fourth", align_bytes=64)
+
+        def sum_corners(relaid, t, k):
+            for j in range(K):
+                nc.tensor.matmul(
+                    sums[k][:, t, :], relaid[:, j, :], ident[:], start=(j == 0), stop=(j == K - 1), is_transpose=True
+                )
+            turned = ring.tile([P, P], F32, name="turned")
+            nc.scalar.copy(turned[:], sums[k][:, t, :])
+            return turned, t, k
+
+        def turn_back(turned, t, k):
+            nc.tensor.transpose(backs[k][:, t, :], turned[:], ident[:])
+            if (t, k) == (2, 3):
+                nc.scalar.copy(last_e[:, 0:3, :], backs[3][:, 0:3, :])
+                nc.scalar.copy(fourth[:], last_e[:].rearrange("p t g -> p g t"))
+
+        waiting = []
+        for t in range(PACK):
+            e0 = 0
+            for piece in PIECES[t]:
+                prod = wide.tile([P, piece], F32, name=f"prod_{piece}")
+                nc.vector.tensor_tensor(
+                    prod[:],
+                    planes[t][:].indirect(offsets[:, e0 // 16 : (e0 + piece) // 16]),
+                    part_rep[:, e0 : e0 + piece],
+                    MULT,
+                )
+                for c in range(piece // 512):
+                    k = e0 // 512 + c
+                    if t == 3 and k == 3:
+                        continue
+                    waiting.append(
+                        sum_corners(prod[:, c * 512 : (c + 1) * 512].rearrange("p (g j) -> p j g", j=K), t, k)
+                    )
+                    if len(waiting) > 1:
+                        turn_back(*waiting.pop(0))
+                    if (t, k) == (3, 0):
+                        nc.scalar.copy(w_grouped[:], w_raw[:].rearrange("p t m -> p m t"))
+                e0 += piece
+        turn_back(*waiting.pop(0))
+
+        pair = held.tile([P, 2, P, PACK], BF16, name="pair", align_bytes=64)
+        third = held.tile([P, P, PACK], BF16, name="third", align_bytes=64)
+
+        def quantize(flat, name):
+            n = flat.shape[1] // PACK
+            codes = held.tile([P, n], U32, name=f"codes{name}", align_bytes=64)
+            scales = held.tile([P, n], U8, name=f"scales{name}", align_bytes=64)
+            nc.vector.quantize_mx(out=codes[:].bitcast(FP8X4), scales=scales[:], in_=flat)
+            return codes, scales
+
+        def multiply(k, codes, scales):
+            acc = psum.tile([P, 2, P], F32, name=f"acc{k}", tag=f"fore{k}")
+            for m in range(2):
+                cols = slice(m * P, (m + 1) * P)
+                nc.tensor.matmul_mx(
+                    out=acc[:, m, :],
+                    lhsT=w_codes[:, cols].bitcast(FP8X4),
+                    lhsT_scale=w_scales[:, cols],
+                    rhs=codes.bitcast(FP8X4),
+                    rhs_scale=scales,
+                    start=True,
+                    stop=True,
+                )
+            result = held.tile([P, 2, P], F32, name=f"result{k}")
+            if k < 2:
+                nc.scalar.copy(result[:], acc[:])
+            elif k == 3:
+                nc.vector.tensor_copy(result[:], acc[:])
+            else:
+                nc.scalar.copy(result[:, 0, :], acc[:, 0, :])
+                nc.vector.tensor_copy(result[:, 1, :], acc[:, 1, :])
+            nc.sync.dma_start(out[:, k * P : (k + 1) * P].rearrange("(m p) g -> p m g", m=2), result[:])
+
+        with nc.allow_low_precision(reason="the float32 sum of four products is rounded to bfloat16 once, on the way out"):
+            nc.vector.tensor_reduce(
+                fourth[:, :, 3], prod[:].rearrange("p (g j) -> p g j", j=K), mybir.AxisListType.X, ADD
+            )
+        nc.vector.quantize_mx(
+            out=w_codes[:].bitcast(FP8X4), scales=w_scales[:], in_=w_grouped[:].rearrange("p m t -> p (m t)")
+        )
+        for k in range(2):
+            nc.scalar.copy(pair[:, k], backs[k][:].rearrange("p t g -> p g t"))
+        nc.scalar.copy(third[:], backs[2][:].rearrange("p t g -> p g t"))
+        c01, s01 = quantize(pair[:].rearrange("p k g t -> p (k g t)"), "01")
+        c3, s3 = quantize(fourth[:].rearrange("p g t -> p (g t)"), "3")
+        c2, s2 = quantize(third[:].rearrange("p g t -> p (g t)"), "2")
+        multiply(0, c01[:, :P], s01[:, :P])
+        multiply(1, c01[:, P:], s01[:, P:])
+        multiply(3, c3[:], s3[:])
+        multiply(2, c2[:], s2[:])

@@ -21,8 +21,11 @@ K = 4
 E = G * K
 PACK = 4
 FLOPS = 2 * D * M * G
+CHUNKS = G // P
+PIECE = P * K
 
-PIECES = ((1024, 1024), (1024, 1024), (1024, 512, 512), (512, 512, 512, 512))
+SHARED = 2
+COPY = mybir.ActivationFunctionType.Copy
 
 
 def tile_attend_grid_kernel(tc, xT, w, part, offs, out):
@@ -31,7 +34,6 @@ def tile_attend_grid_kernel(tc, xT, w, part, offs, out):
     with ExitStack() as ctx:
         held = ctx.enter_context(tc.tile_pool(name="held", bufs=1))
         ring = ctx.enter_context(tc.tile_pool(name="ring", bufs=4))
-        wide = ctx.enter_context(tc.tile_pool(name="wide", bufs=3))
         psum = ctx.enter_context(tc.psum_pool(name="psum", bufs=1))
 
         offsets = held.tile([P, E // 16], U16, name="offsets")
@@ -41,11 +43,12 @@ def tile_attend_grid_kernel(tc, xT, w, part, offs, out):
         planes = []
         for t in range(PACK):
             plane = held.tile([P, T], F32, name=f"plane{t}")
-            for h in range(2):
-                cols = slice(h * T // 2, (h + 1) * T // 2)
+            loads = 4 if t == SHARED else 1
+            for h in range(loads):
+                cols = slice(h * T // loads, (h + 1) * T // loads)
                 nc.sync.dma_start(plane[:, cols], x_planes[:, t, cols])
             planes.append(plane)
-        w_raw = held.tile([P, PACK, M], F32, name="w_raw")
+        w_raw = held.tile([P, PACK, M], F32, name="w_raw", tag="w_raw")
         nc.sync.dma_start(w_raw[:], w.rearrange("(p t) m -> p t m", t=PACK))
 
         ident = held.tile([P, P], F32, name="ident")
@@ -65,58 +68,75 @@ def tile_attend_grid_kernel(tc, xT, w, part, offs, out):
             else:
                 nc.scalar.copy(dst, src)
 
-        sums = [psum.tile([P, PACK, P], F32, name=f"sums{k}", tag=f"fore{k}") for k in range(4)]
-        backs = [psum.tile([P, PACK, P], F32, name=f"backs{k}", tag=f"back{k}") for k in range(4)]
+        sums = [psum.tile([P, PACK, P], F32, name=f"sums{k}", tag=f"fore{k}") for k in range(CHUNKS)]
+        backs = [psum.tile([P, 2, P], F32, name=f"backs{k}", tag=f"back{k}") for k in range(CHUNKS)]
 
-        w_grouped = held.tile([P, M, PACK], BF16, name="w_grouped", align_bytes=64)
+        w_grouped = held.tile([P, M, PACK], BF16, name="w_grouped", tag="w_grouped", align_bytes=64)
         w_codes = held.tile([P, M], U32, name="w_codes", align_bytes=64)
         w_scales = held.tile([P, M], U8, name="w_scales", align_bytes=64)
-        last_e = held.tile([P, PACK, P], F32, name="last_e")
-        nc.gpsimd.memset(last_e[:, 3, :], 0.0)
-        fourth = held.tile([P, P, PACK], BF16, name="fourth", align_bytes=64)
+        first = held.tile([P, P * PACK], BF16, name="first", tag="first", align_bytes=64)
+        second = held.tile([P, P * PACK], BF16, name="second", align_bytes=64)
+        late = held.tile([P, 2, P * PACK], BF16, name="late", align_bytes=64)
+        grouped = [first[:], second[:], late[:, 0, :], late[:, 1, :]]
 
-        def sum_corners(relaid, t, k):
+        def gather(prod, t, e0):
+            n = prod.shape[1]
+            nc.vector.tensor_tensor(
+                prod[:], planes[t][:].indirect(offsets[:, e0 // 16 : (e0 + n) // 16]), part_rep[:, e0 : e0 + n], MULT
+            )
+
+        def sum_corners(prod, t, k):
+            corners = prod[:].rearrange("p (g j) -> p j g", j=K)
             for j in range(K):
                 nc.tensor.matmul(
-                    sums[k][:, t, :], relaid[:, j, :], ident[:], start=(j == 0), stop=(j == K - 1), is_transpose=True
+                    sums[k][:, t, :], corners[:, j, :], ident[:], start=(j == 0), stop=(j == K - 1), is_transpose=True
                 )
-            turned = ring.tile([P, P], F32, name="turned")
-            nc.scalar.copy(turned[:], sums[k][:, t, :])
-            return turned, t, k
 
-        def turn_back(turned, t, k):
-            nc.tensor.transpose(backs[k][:, t, :], turned[:], ident[:])
-            if (t, k) == (2, 3):
-                nc.scalar.copy(last_e[:, 0:3, :], backs[3][:, 0:3, :])
-                nc.scalar.copy(fourth[:], last_e[:].rearrange("p t g -> p g t"))
+        def round_pair(turned, src, u, k):
+            nc.scalar.copy(turned, src)
+            return turned, u, k
+
+        def turn_back(turned, u, k):
+            nc.tensor.transpose(backs[k][:, u, :], turned.rearrange("g p e -> g (p e)").bitcast(F32), ident[:])
+            if u == 1:
+                nc.scalar.copy(
+                    grouped[k].bitcast(F32).rearrange("p (g u) -> p g u", u=2), backs[k][:].rearrange("p u g -> p g u")
+                )
+
+        narrow = held.tile([P, T], BF16, name="narrow", tag="narrow")
+        for t in range(SHARED + 1):
+            if t == SHARED:
+                for h in range(4):
+                    cols = slice(h * T // 4, (h + 1) * T // 4)
+                    nc.scalar.activation(narrow[:, cols], planes[t][:, cols], COPY)
+            for k in range(CHUNKS):
+                prod = ring.tile([P, PIECE], F32, name="prod")
+                if t == SHARED and k >= 2:
+                    picked = ring.tile([P, PIECE], BF16, name="picked")
+                    entries = offsets[:, k * PIECE // 16 : (k + 1) * PIECE // 16]
+                    nc.scalar.activation(picked[:], narrow[:].indirect(entries), COPY)
+                    nc.vector.tensor_tensor(prod[:], picked[:], part_rep[:, k * PIECE : (k + 1) * PIECE], MULT)
+                else:
+                    gather(prod, t, k * PIECE)
+                sum_corners(prod, t, k)
+
+        early = held.tile([P, CHUNKS, P, 2], BF16, name="early", tag="narrow")
+        for k in range(CHUNKS):
+            turn_back(*round_pair(early[:, k], sums[k][:, 0:2, :].rearrange("g e p -> g p e"), 0, k))
+        turned = ring.tile([P, P, 2], BF16, name="turned")
+        turn_back(*round_pair(turned[:], sums[3][:, 2, :].unsqueeze(2).to_broadcast([P, P, 2]), 1, 3))
+        nc.scalar.copy(w_grouped[:], w_raw[:].rearrange("p t m -> p m t"))
 
         waiting = []
-        for t in range(PACK):
-            e0 = 0
-            for piece in PIECES[t]:
-                prod = wide.tile([P, piece], F32, name=f"prod_{piece}")
-                nc.vector.tensor_tensor(
-                    prod[:],
-                    planes[t][:].indirect(offsets[:, e0 // 16 : (e0 + piece) // 16]),
-                    part_rep[:, e0 : e0 + piece],
-                    MULT,
-                )
-                for c in range(piece // 512):
-                    k = e0 // 512 + c
-                    if t == 3 and k == 3:
-                        continue
-                    waiting.append(
-                        sum_corners(prod[:, c * 512 : (c + 1) * 512].rearrange("p (g j) -> p j g", j=K), t, k)
-                    )
-                    if len(waiting) > 1:
-                        turn_back(*waiting.pop(0))
-                    if (t, k) == (3, 0):
-                        nc.scalar.copy(w_grouped[:], w_raw[:].rearrange("p t m -> p m t"))
-                e0 += piece
-        turn_back(*waiting.pop(0))
-
-        pair = held.tile([P, 2, P, PACK], BF16, name="pair", align_bytes=64)
-        third = held.tile([P, P, PACK], BF16, name="third", align_bytes=64)
+        for k in range(CHUNKS - 1):
+            prod = ring.tile([P, PIECE], F32, name="prod")
+            gather(prod, 3, k * PIECE)
+            sum_corners(prod, 3, k)
+            if waiting:
+                turn_back(*waiting.pop())
+            turned = ring.tile([P, P, 2], BF16, name="turned")
+            waiting.append(round_pair(turned[:], sums[k][:, 2:4, :].rearrange("g e p -> g p e"), 1, k))
+        turn_back(*waiting.pop())
 
         def quantize(flat, name):
             n = flat.shape[1] // PACK
@@ -125,43 +145,51 @@ def tile_attend_grid_kernel(tc, xT, w, part, offs, out):
             nc.vector.quantize_mx(out=codes[:].bitcast(FP8X4), scales=scales[:], in_=flat)
             return codes, scales
 
-        def multiply(k, codes, scales):
+        def multiply(acc, m, codes, scales):
+            cols = slice(m * P, (m + 1) * P)
+            nc.tensor.matmul_mx(
+                out=acc,
+                lhsT=w_codes[:, cols].bitcast(FP8X4),
+                lhsT_scale=w_scales[:, cols],
+                rhs=codes[:].bitcast(FP8X4),
+                rhs_scale=scales[:],
+                start=True,
+                stop=True,
+            )
+
+        def reduce_corners(prod, g0):
+            n = prod.shape[1] // K
+            with nc.allow_low_precision(reason="the float32 sum of four products is rounded to bfloat16 once"):
+                nc.vector.tensor_reduce(
+                    grouped[3].rearrange("p (g t) -> p g t", t=PACK)[:, g0 : g0 + n, 3],
+                    prod[:].rearrange("p (g j) -> p g j", j=K),
+                    mybir.AxisListType.X,
+                    ADD,
+                )
+
+        def finish(k, codes, scales):
             acc = psum.tile([P, 2, P], F32, name=f"acc{k}", tag=f"fore{k}")
             for m in range(2):
-                cols = slice(m * P, (m + 1) * P)
-                nc.tensor.matmul_mx(
-                    out=acc[:, m, :],
-                    lhsT=w_codes[:, cols].bitcast(FP8X4),
-                    lhsT_scale=w_scales[:, cols],
-                    rhs=codes.bitcast(FP8X4),
-                    rhs_scale=scales,
-                    start=True,
-                    stop=True,
-                )
+                multiply(acc[:, m, :], m, codes, scales)
             result = held.tile([P, 2, P], F32, name=f"result{k}")
-            if k < 2:
-                nc.scalar.copy(result[:], acc[:])
-            elif k == 3:
-                nc.vector.tensor_copy(result[:], acc[:])
-            else:
-                nc.scalar.copy(result[:, 0, :], acc[:, 0, :])
-                nc.vector.tensor_copy(result[:, 1, :], acc[:, 1, :])
+            nc.scalar.copy(result[:], acc[:])
             nc.sync.dma_start(out[:, k * P : (k + 1) * P].rearrange("(m p) g -> p m g", m=2), result[:])
 
-        with nc.allow_low_precision(reason="the float32 sum of four products is rounded to bfloat16 once, on the way out"):
-            nc.vector.tensor_reduce(
-                fourth[:, :, 3], prod[:].rearrange("p (g j) -> p g j", j=K), mybir.AxisListType.X, ADD
-            )
+        prod = ring.tile([P, PIECE], F32, name="prod")
+        gather(prod, 3, 3 * PIECE)
+        reduce_corners(prod, 0)
         nc.vector.quantize_mx(
             out=w_codes[:].bitcast(FP8X4), scales=w_scales[:], in_=w_grouped[:].rearrange("p m t -> p (m t)")
         )
-        for k in range(2):
-            nc.scalar.copy(pair[:, k], backs[k][:].rearrange("p t g -> p g t"))
-        nc.scalar.copy(third[:], backs[2][:].rearrange("p t g -> p g t"))
-        c01, s01 = quantize(pair[:].rearrange("p k g t -> p (k g t)"), "01")
-        c3, s3 = quantize(fourth[:].rearrange("p g t -> p (g t)"), "3")
-        c2, s2 = quantize(third[:].rearrange("p g t -> p (g t)"), "2")
-        multiply(0, c01[:, :P], s01[:, :P])
-        multiply(1, c01[:, P:], s01[:, P:])
-        multiply(3, c3[:], s3[:])
-        multiply(2, c2[:], s2[:])
+        finish(0, *quantize(grouped[0], "0"))
+        finish(1, *quantize(grouped[1], "1"))
+        c23, s23 = quantize(late[:].rearrange("p k n -> p (k n)"), "23")
+        for m, bank in enumerate(("fore3", "back3")):
+            acc = psum.tile([P, 2 * P], F32, name=f"acc23_{m}", tag=bank)
+            multiply(acc[:], m, c23, s23)
+            result = held.tile([P, 2 * P], F32, name=f"result23_{m}")
+            if m == 0:
+                nc.scalar.copy(result[:], acc[:])
+            else:
+                nc.vector.tensor_copy(result[:], acc[:])
+            nc.sync.dma_start(out[m * P : (m + 1) * P, 2 * P :], result[:])

@@ -74,10 +74,9 @@ def tile_attend_grid_kernel(tc, xT, w, part, offs, out):
         w_grouped = held.tile([P, M, PACK], BF16, name="w_grouped", tag="w_grouped", align_bytes=64)
         w_codes = held.tile([P, M], U32, name="w_codes", align_bytes=64)
         w_scales = held.tile([P, M], U8, name="w_scales", align_bytes=64)
-        first = held.tile([P, P * PACK], BF16, name="first", tag="first", align_bytes=64)
-        second = held.tile([P, P * PACK], BF16, name="second", align_bytes=64)
-        late = held.tile([P, 2, P * PACK], BF16, name="late", align_bytes=64)
-        grouped = [first[:], second[:], late[:, 0, :], late[:, 1, :]]
+        grouped = [
+            held.tile([P, P * PACK], BF16, name=f"grouped{k}", tag=f"grouped{k}", align_bytes=64)[:] for k in range(CHUNKS)
+        ]
 
         def gather(prod, t, e0):
             n = prod.shape[1]
@@ -85,8 +84,7 @@ def tile_attend_grid_kernel(tc, xT, w, part, offs, out):
                 prod[:], planes[t][:].indirect(offsets[:, e0 // 16 : (e0 + n) // 16]), part_rep[:, e0 : e0 + n], MULT
             )
 
-        def sum_corners(prod, t, k):
-            corners = prod[:].rearrange("p (g j) -> p j g", j=K)
+        def sum_corners(corners, t, k):
             for j in range(K):
                 nc.tensor.matmul(
                     sums[k][:, t, :], corners[:, j, :], ident[:], start=(j == 0), stop=(j == K - 1), is_transpose=True
@@ -103,44 +101,52 @@ def tile_attend_grid_kernel(tc, xT, w, part, offs, out):
                     grouped[k].bitcast(F32).rearrange("p (g u) -> p g u", u=2), backs[k][:].rearrange("p u g -> p g u")
                 )
 
+        part_apart = held.tile([P, 2, K, P], F32, name="part_apart")
+        nc.vector.tensor_copy(part_apart[:], part_rep[:, : 2 * PIECE].rearrange("p (k g j) -> p k j g", k=2, j=K))
+
+        def gather_chunk(t, k):
+            prod = ring.tile([P, PIECE], F32, name="prod")
+            gather(prod, t, k * PIECE)
+            return prod[:].rearrange("p (g j) -> p j g", j=K)
+
         narrow = held.tile([P, T], BF16, name="narrow", tag="narrow")
         for t in range(SHARED + 1):
             if t == SHARED:
                 for h in range(4):
                     cols = slice(h * T // 4, (h + 1) * T // 4)
                     nc.scalar.activation(narrow[:, cols], planes[t][:, cols], COPY)
-            for k in range(CHUNKS):
-                prod = ring.tile([P, PIECE], F32, name="prod")
-                if t == SHARED and k >= 2:
-                    picked = ring.tile([P, PIECE], BF16, name="picked")
+            for k in (3, 2, 0, 1) if t == SHARED else range(CHUNKS):
+                if t == SHARED and k < 2:
+                    picked = ring.tile([P, K, P], BF16, name="picked")
                     entries = offsets[:, k * PIECE // 16 : (k + 1) * PIECE // 16]
-                    nc.scalar.activation(picked[:], narrow[:].indirect(entries), COPY)
-                    nc.vector.tensor_tensor(prod[:], picked[:], part_rep[:, k * PIECE : (k + 1) * PIECE], MULT)
+                    nc.scalar.activation(picked[:].rearrange("p j g -> p g j"), narrow[:].indirect(entries), COPY)
+                    prod = ring.tile([P, K, P], F32, name="prod")
+                    nc.vector.tensor_tensor(prod[:], picked[:], part_apart[:, k], MULT)
+                    corners = prod[:]
                 else:
-                    gather(prod, t, k * PIECE)
-                sum_corners(prod, t, k)
+                    corners = gather_chunk(t, k)
+                sum_corners(corners, t, k)
 
         early = held.tile([P, CHUNKS, P, 2], BF16, name="early", tag="narrow")
-        for k in range(CHUNKS):
+        for k in (3, 2, 0, 1):
             turn_back(*round_pair(early[:, k], sums[k][:, 0:2, :].rearrange("g e p -> g p e"), 0, k))
-        turned = ring.tile([P, P, 2], BF16, name="turned")
-        turn_back(*round_pair(turned[:], sums[3][:, 2, :].unsqueeze(2).to_broadcast([P, P, 2]), 1, 3))
+            if k == 3:
+                turned = ring.tile([P, P, 2], BF16, name="turned")
+                turn_back(*round_pair(turned[:], sums[k][:, 2, :].unsqueeze(2).to_broadcast([P, P, 2]), 1, k))
         nc.scalar.copy(w_grouped[:], w_raw[:].rearrange("p t m -> p m t"))
 
         waiting = []
         for k in range(CHUNKS - 1):
-            prod = ring.tile([P, PIECE], F32, name="prod")
-            gather(prod, 3, k * PIECE)
-            sum_corners(prod, 3, k)
+            sum_corners(gather_chunk(3, k), 3, k)
             if waiting:
                 turn_back(*waiting.pop())
             turned = ring.tile([P, P, 2], BF16, name="turned")
             waiting.append(round_pair(turned[:], sums[k][:, 2:4, :].rearrange("g e p -> g p e"), 1, k))
         turn_back(*waiting.pop())
 
-        def quantize(flat, name):
+        def quantize(flat, name, tag=None):
             n = flat.shape[1] // PACK
-            codes = held.tile([P, n], U32, name=f"codes{name}", align_bytes=64)
+            codes = held.tile([P, n], U32, name=f"codes{name}", tag=tag or f"codes{name}", align_bytes=64)
             scales = held.tile([P, n], U8, name=f"scales{name}", align_bytes=64)
             nc.vector.quantize_mx(out=codes[:].bitcast(FP8X4), scales=scales[:], in_=flat)
             return codes, scales
@@ -157,11 +163,11 @@ def tile_attend_grid_kernel(tc, xT, w, part, offs, out):
                 stop=True,
             )
 
-        def reduce_corners(prod, g0):
+        def reduce_corners(prod, k, g0):
             n = prod.shape[1] // K
             with nc.allow_low_precision(reason="the float32 sum of four products is rounded to bfloat16 once"):
                 nc.vector.tensor_reduce(
-                    grouped[3].rearrange("p (g t) -> p g t", t=PACK)[:, g0 : g0 + n, 3],
+                    grouped[k].rearrange("p (g t) -> p g t", t=PACK)[:, g0 : g0 + n, 3],
                     prod[:].rearrange("p (g j) -> p g j", j=K),
                     mybir.AxisListType.X,
                     ADD,
@@ -172,24 +178,28 @@ def tile_attend_grid_kernel(tc, xT, w, part, offs, out):
             for m in range(2):
                 multiply(acc[:, m, :], m, codes, scales)
             result = held.tile([P, 2, P], F32, name=f"result{k}")
-            nc.scalar.copy(result[:], acc[:])
+            if k == 3:
+                nc.vector.tensor_copy(result[:], acc[:])
+            else:
+                nc.scalar.copy(result[:], acc[:])
             nc.sync.dma_start(out[:, k * P : (k + 1) * P].rearrange("(m p) g -> p m g", m=2), result[:])
 
-        prod = ring.tile([P, PIECE], F32, name="prod")
-        gather(prod, 3, 3 * PIECE)
-        reduce_corners(prod, 0)
         nc.vector.quantize_mx(
             out=w_codes[:].bitcast(FP8X4), scales=w_scales[:], in_=w_grouped[:].rearrange("p m t -> p (m t)")
         )
+        prod = held.tile([P, PIECE], F32, name="last_prod", tag="w_grouped", align_bytes=64)
+        gather(prod, 3, 3 * PIECE)
         finish(0, *quantize(grouped[0], "0"))
+        reduce_corners(prod, 3, 0)
         finish(1, *quantize(grouped[1], "1"))
-        c23, s23 = quantize(late[:].rearrange("p k n -> p (k n)"), "23")
-        for m, bank in enumerate(("fore3", "back3")):
-            acc = psum.tile([P, 2 * P], F32, name=f"acc23_{m}", tag=bank)
-            multiply(acc[:], m, c23, s23)
-            result = held.tile([P, 2 * P], F32, name=f"result23_{m}")
+        finish(3, *quantize(grouped[3], "3"))
+        c2, s2 = quantize(grouped[2], "2")
+        result = held.tile([P, 2, P], F32, name="result2")
+        for m, bank in enumerate(("fore2", "back3")):
+            acc = psum.tile([P, P], F32, name=f"acc2_{m}", tag=bank)
+            multiply(acc[:], m, c2, s2)
             if m == 0:
-                nc.scalar.copy(result[:], acc[:])
+                nc.scalar.copy(result[:, m, :], acc[:])
             else:
-                nc.vector.tensor_copy(result[:], acc[:])
-            nc.sync.dma_start(out[m * P : (m + 1) * P, 2 * P :], result[:])
+                nc.vector.tensor_copy(result[:, m, :], acc[:])
+        nc.sync.dma_start(out[:, 2 * P : 3 * P].rearrange("(m p) g -> p m g", m=2), result[:])

@@ -34,6 +34,7 @@ def tile_attend_grid_kernel(tc, xT, w, part, offs, out):
     with ExitStack() as ctx:
         held = ctx.enter_context(tc.tile_pool(name="held", bufs=1))
         ring = ctx.enter_context(tc.tile_pool(name="ring", bufs=4))
+        wide = ctx.enter_context(tc.tile_pool(name="wide", bufs=3))
         psum = ctx.enter_context(tc.psum_pool(name="psum", bufs=1))
 
         offsets = held.tile([P, E // 16], U16, name="offsets")
@@ -109,23 +110,31 @@ def tile_attend_grid_kernel(tc, xT, w, part, offs, out):
             gather(prod, t, k * PIECE)
             return prod[:].rearrange("p (g j) -> p j g", j=K)
 
+        for t in range(SHARED):
+            for half in range(2):
+                prod = wide.tile([P, 2 * PIECE], F32, name="wide_prod")
+                gather(prod, t, half * 2 * PIECE)
+                for c in range(2):
+                    corners = prod[:, c * PIECE : (c + 1) * PIECE].rearrange("p (g j) -> p j g", j=K)
+                    sum_corners(corners, t, 2 * half + c)
+
         narrow = held.tile([P, T], BF16, name="narrow", tag="narrow")
-        for t in range(SHARED + 1):
-            if t == SHARED:
-                for h in range(4):
-                    cols = slice(h * T // 4, (h + 1) * T // 4)
-                    nc.scalar.activation(narrow[:, cols], planes[t][:, cols], COPY)
-            for k in (3, 2, 0, 1) if t == SHARED else range(CHUNKS):
-                if t == SHARED and k < 2:
-                    picked = ring.tile([P, K, P], BF16, name="picked")
-                    entries = offsets[:, k * PIECE // 16 : (k + 1) * PIECE // 16]
-                    nc.scalar.activation(picked[:].rearrange("p j g -> p g j"), narrow[:].indirect(entries), COPY)
-                    prod = ring.tile([P, K, P], F32, name="prod")
-                    nc.vector.tensor_tensor(prod[:], picked[:], part_apart[:, k], MULT)
-                    corners = prod[:]
-                else:
-                    corners = gather_chunk(t, k)
-                sum_corners(corners, t, k)
+        for h in range(4):
+            cols = slice(h * T // 4, (h + 1) * T // 4)
+            nc.scalar.activation(narrow[:, cols], planes[SHARED][:, cols], COPY)
+        for k in (3, 2):
+            sum_corners(gather_chunk(SHARED, k), SHARED, k)
+        for k, parts in ((0, 1), (1, 2)):
+            prod = ring.tile([P, K, P], F32, name="prod")
+            for h in range(parts):
+                n = P // parts
+                picked = ring.tile([P, n * K], BF16, name="picked")
+                e0 = k * PIECE + h * n * K
+                entries = offsets[:, e0 // 16 : (e0 + n * K) // 16]
+                nc.scalar.activation(picked[:], narrow[:].indirect(entries), COPY)
+                points = slice(h * n, (h + 1) * n)
+                nc.vector.tensor_tensor(prod[:, :, points], picked[:].rearrange("p (g j) -> p j g", j=K), part_apart[:, k, :, points], MULT)
+            sum_corners(prod[:], SHARED, k)
 
         early = held.tile([P, CHUNKS, P, 2], BF16, name="early", tag="narrow")
         for k in (3, 2, 0, 1):
@@ -178,7 +187,7 @@ def tile_attend_grid_kernel(tc, xT, w, part, offs, out):
             for m in range(2):
                 multiply(acc[:, m, :], m, codes, scales)
             result = held.tile([P, 2, P], F32, name=f"result{k}")
-            if k == 3:
+            if k == 1:
                 nc.vector.tensor_copy(result[:], acc[:])
             else:
                 nc.scalar.copy(result[:], acc[:])
@@ -188,11 +197,13 @@ def tile_attend_grid_kernel(tc, xT, w, part, offs, out):
             out=w_codes[:].bitcast(FP8X4), scales=w_scales[:], in_=w_grouped[:].rearrange("p m t -> p (m t)")
         )
         prod = held.tile([P, PIECE], F32, name="last_prod", tag="w_grouped", align_bytes=64)
-        gather(prod, 3, 3 * PIECE)
-        finish(0, *quantize(grouped[0], "0"))
-        reduce_corners(prod, 3, 0)
-        finish(1, *quantize(grouped[1], "1"))
-        finish(3, *quantize(grouped[3], "3"))
+        halves = [prod[:, h * PIECE // 2 : (h + 1) * PIECE // 2] for h in range(2)]
+        for h in range(2):
+            gather(halves[h], 3, 3 * PIECE + h * PIECE // 2)
+        for h in range(2):
+            reduce_corners(halves[h], 3, h * P // 2)
+        for k in (0, 3, 1):
+            finish(k, *quantize(grouped[k], str(k)))
         c2, s2 = quantize(grouped[2], "2")
         result = held.tile([P, 2, P], F32, name="result2")
         for m, bank in enumerate(("fore2", "back3")):

@@ -41,6 +41,8 @@ def tile_attend_grid_kernel(tc, xT, w, part, offs, out):
         nc.sync.dma_start(offsets[:], offs)
         part_col = held.tile([P, E // P], F32, name="part_col")
         nc.scalar.dma_start(part_col[:], part[0:1, :].rearrange("o (q i) -> (o q) i", i=E // P))
+        part_last = held.tile([P, K], F32, name="part_last")
+        nc.scalar.dma_start(part_last[:], part[0:1, 3 * PIECE :].rearrange("o (g j) -> (o g) j", j=K))
         planes = []
         for t in range(PACK):
             plane = held.tile([P, T], F32, name=f"plane{t}")
@@ -49,11 +51,13 @@ def tile_attend_grid_kernel(tc, xT, w, part, offs, out):
                 cols = slice(h * T // loads, (h + 1) * T // loads)
                 nc.sync.dma_start(plane[:, cols], x_planes[:, t, cols])
             planes.append(plane)
-        w_raw = held.tile([P, PACK, M], F32, name="w_raw", tag="w_raw")
+        w_raw = held.tile([P, PACK, M], F32, name="w_raw", tag="w_raw", align_bytes=64)
         nc.sync.dma_start(w_raw[:], w.rearrange("(p t) m -> p t m", t=PACK))
 
         ident = held.tile([P, P], F32, name="ident")
         make_identity(nc, ident[:])
+        ident_narrow = held.tile([P, P], BF16, name="ident_narrow")
+        make_identity(nc, ident_narrow[:])
 
         part_rep = held.tile([P, E], F32, name="part_rep")
         part_view = part_rep[:].rearrange("p (q i) -> p q i", i=E // P)
@@ -69,26 +73,28 @@ def tile_attend_grid_kernel(tc, xT, w, part, offs, out):
             else:
                 nc.scalar.copy(dst, src)
 
-        sums = [psum.tile([P, PACK, P], F32, name=f"sums{k}", tag=f"fore{k}") for k in range(CHUNKS)]
-        backs = [psum.tile([P, 2, P], F32, name=f"backs{k}", tag=f"back{k}") for k in range(CHUNKS)]
+        first = [psum.tile([P, PACK, P], F32, name=f"first{k}", tag=f"back{k}") for k in range(CHUNKS)]
+        second = [psum.tile([P, 2, P], F32, name=f"second{k}", tag=f"fore{k}") for k in range(CHUNKS - 1)]
+        sums = [(first[k][:, 0:2, :], second[k][:] if k < CHUNKS - 1 else None) for k in range(CHUNKS)]
+        backs = [first[k][:, 2:4, :] for k in range(CHUNKS)]
 
         w_grouped = held.tile([P, M, PACK], BF16, name="w_grouped", tag="w_grouped", align_bytes=64)
         w_codes = held.tile([P, M], U32, name="w_codes", align_bytes=64)
         w_scales = held.tile([P, M], U8, name="w_scales", align_bytes=64)
         grouped = [
-            held.tile([P, P * PACK], BF16, name=f"grouped{k}", tag=f"grouped{k}", align_bytes=64)[:] for k in range(CHUNKS)
+            held.tile([P, P * PACK], BF16, name=f"grouped{k}", tag=f"grouped{k}", align_bytes=64)[:] for k in range(2)
         ]
 
         def gather(prod, t, e0):
             n = prod.shape[1]
             nc.vector.tensor_tensor(
-                prod[:], planes[t][:].indirect(offsets[:, e0 // 16 : (e0 + n) // 16]), part_rep[:, e0 : e0 + n], MULT
+                prod, planes[t][:].indirect(offsets[:, e0 // 16 : (e0 + n) // 16]), part_rep[:, e0 : e0 + n], MULT
             )
 
         def sum_corners(corners, t, k):
             for j in range(K):
                 nc.tensor.matmul(
-                    sums[k][:, t, :], corners[:, j, :], ident[:], start=(j == 0), stop=(j == K - 1), is_transpose=True
+                    sums[k][t // 2][:, t % 2, :], corners[:, j, :], ident[:], start=(j == 0), stop=(j == K - 1), is_transpose=True
                 )
 
         def round_pair(turned, src, u, k):
@@ -98,22 +104,18 @@ def tile_attend_grid_kernel(tc, xT, w, part, offs, out):
         def turn_back(turned, u, k):
             nc.tensor.transpose(backs[k][:, u, :], turned.rearrange("g p e -> g (p e)").bitcast(F32), ident[:])
             if u == 1:
-                nc.scalar.copy(
-                    grouped[k].bitcast(F32).rearrange("p (g u) -> p g u", u=2), backs[k][:].rearrange("p u g -> p g u")
-                )
-
-        part_apart = held.tile([P, 2, K, P], F32, name="part_apart")
-        nc.vector.tensor_copy(part_apart[:], part_rep[:, : 2 * PIECE].rearrange("p (k g j) -> p k j g", k=2, j=K))
+                words = grouped[k].bitcast(F32).rearrange("p (g u) -> p g u", u=2)
+                nc.scalar.copy(words, backs[k].rearrange("p u g -> p g u"))
 
         def gather_chunk(t, k):
             prod = ring.tile([P, PIECE], F32, name="prod")
-            gather(prod, t, k * PIECE)
+            gather(prod[:], t, k * PIECE)
             return prod[:].rearrange("p (g j) -> p j g", j=K)
 
         for t in range(SHARED):
             for half in range(2):
                 prod = wide.tile([P, 2 * PIECE], F32, name="wide_prod")
-                gather(prod, t, half * 2 * PIECE)
+                gather(prod[:], t, half * 2 * PIECE)
                 for c in range(2):
                     corners = prod[:, c * PIECE : (c + 1) * PIECE].rearrange("p (g j) -> p j g", j=K)
                     sum_corners(corners, t, 2 * half + c)
@@ -122,42 +124,41 @@ def tile_attend_grid_kernel(tc, xT, w, part, offs, out):
         for h in range(4):
             cols = slice(h * T // 4, (h + 1) * T // 4)
             nc.scalar.activation(narrow[:, cols], planes[SHARED][:, cols], COPY)
-        for k in (3, 2):
+        for k in (2, 0):
             sum_corners(gather_chunk(SHARED, k), SHARED, k)
-        for k, parts in ((0, 1), (1, 2)):
-            prod = ring.tile([P, K, P], F32, name="prod")
-            for h in range(parts):
-                n = P // parts
-                picked = ring.tile([P, n * K], BF16, name="picked")
-                e0 = k * PIECE + h * n * K
-                entries = offsets[:, e0 // 16 : (e0 + n * K) // 16]
-                nc.scalar.activation(picked[:], narrow[:].indirect(entries), COPY)
-                points = slice(h * n, (h + 1) * n)
-                nc.vector.tensor_tensor(prod[:, :, points], picked[:].rearrange("p (g j) -> p j g", j=K), part_apart[:, k, :, points], MULT)
-            sum_corners(prod[:], SHARED, k)
 
-        early = held.tile([P, CHUNKS, P, 2], BF16, name="early", tag="narrow")
-        for k in (3, 2, 0, 1):
-            turn_back(*round_pair(early[:, k], sums[k][:, 0:2, :].rearrange("g e p -> g p e"), 0, k))
-            if k == 3:
-                turned = ring.tile([P, P, 2], BF16, name="turned")
-                turn_back(*round_pair(turned[:], sums[k][:, 2, :].unsqueeze(2).to_broadcast([P, P, 2]), 1, k))
+        picked = held.tile([P, PIECE], BF16, name="picked")
+        nc.scalar.activation(picked[:], narrow[:].indirect(offsets[:, 3 * PIECE // 16 :]), COPY)
+        corners = psum.tile([P, K, P], BF16, name="corners", tag="fore3")
+        for j in range(K):
+            nc.tensor.transpose(corners[:, j, :], picked[:].rearrange("p (g j) -> p j g", j=K)[:, j, :], ident_narrow[:])
+        after_narrow = held.tile([P, 2 * PIECE], F32, name="after_narrow", tag="narrow")
+        gather(after_narrow[:, :PIECE], SHARED, PIECE)
+        sum_corners(after_narrow[:, :PIECE].rearrange("p (g j) -> p j g", j=K), SHARED, 1)
+        weighed = held.tile([P, K, P], F32, name="weighed")
+        for j in range(K):
+            nc.scalar.activation(weighed[:, j, :], corners[:, j, :], COPY, scale=part_last[:, j : j + 1])
+        direct = psum.tile([P, P], F32, name="direct", tag="fore3")
+        for j in range(K):
+            nc.tensor.matmul(direct[:], weighed[:, j, :], ident[:], start=(j == 0), stop=(j == K - 1), is_transpose=True)
+
+        early = after_narrow[:, PIECE:].bitcast(BF16).rearrange("g (k p e) -> g k p e", k=CHUNKS, e=2)
+        for k in (2, 3, 0, 1):
+            turn_back(*round_pair(early[:, k], sums[k][0].rearrange("g e p -> g p e"), 0, k))
+        doubled = held.tile([P, P, 2], BF16, name="doubled")
+        nc.scalar.copy(doubled[:], sums[2][1][:, 0, :].unsqueeze(2).to_broadcast([P, P, 2]))
+        nc.tensor.transpose(backs[2][:, 1, :], doubled[:].rearrange("g p e -> g (p e)").bitcast(F32), ident[:])
         nc.scalar.copy(w_grouped[:], w_raw[:].rearrange("p t m -> p m t"))
+        after_w = held.tile([P, 2 * P * PACK], BF16, name="after_w", tag="w_raw", align_bytes=64)
+        grouped.extend([after_w[:, : P * PACK], after_w[:, P * PACK :]])
+        nc.scalar.copy(grouped[2].bitcast(F32).rearrange("p (g u) -> p g u", u=2), backs[2].rearrange("p u g -> p g u"))
 
-        waiting = []
-        for k in range(CHUNKS - 1):
-            sum_corners(gather_chunk(3, k), 3, k)
-            if waiting:
-                turn_back(*waiting.pop())
-            turned = ring.tile([P, P, 2], BF16, name="turned")
-            waiting.append(round_pair(turned[:], sums[k][:, 2:4, :].rearrange("g e p -> g p e"), 1, k))
-        turn_back(*waiting.pop())
-
-        def quantize(flat, name, tag=None):
+        def quantize(flat, name, codes=None):
             n = flat.shape[1] // PACK
-            codes = held.tile([P, n], U32, name=f"codes{name}", tag=tag or f"codes{name}", align_bytes=64)
+            if codes is None:
+                codes = held.tile([P, n], U32, name=f"codes{name}", align_bytes=64)[:]
             scales = held.tile([P, n], U8, name=f"scales{name}", align_bytes=64)
-            nc.vector.quantize_mx(out=codes[:].bitcast(FP8X4), scales=scales[:], in_=flat)
+            nc.vector.quantize_mx(out=codes.bitcast(FP8X4), scales=scales[:], in_=flat)
             return codes, scales
 
         def multiply(acc, m, codes, scales):
@@ -166,7 +167,7 @@ def tile_attend_grid_kernel(tc, xT, w, part, offs, out):
                 out=acc,
                 lhsT=w_codes[:, cols].bitcast(FP8X4),
                 lhsT_scale=w_scales[:, cols],
-                rhs=codes[:].bitcast(FP8X4),
+                rhs=codes.bitcast(FP8X4),
                 rhs_scale=scales[:],
                 start=True,
                 stop=True,
@@ -182,35 +183,45 @@ def tile_attend_grid_kernel(tc, xT, w, part, offs, out):
                     ADD,
                 )
 
-        def finish(k, codes, scales):
-            acc = psum.tile([P, 2, P], F32, name=f"acc{k}", tag=f"fore{k}")
+        def finish(name, bank, g0, copy, codes, scales):
+            n = codes.shape[1]
+            acc = psum.tile([P, 2, n], F32, name=f"acc{name}", tag=bank)
             for m in range(2):
                 multiply(acc[:, m, :], m, codes, scales)
-            result = held.tile([P, 2, P], F32, name=f"result{k}")
-            if k == 1:
-                nc.vector.tensor_copy(result[:], acc[:])
-            else:
-                nc.scalar.copy(result[:], acc[:])
-            nc.sync.dma_start(out[:, k * P : (k + 1) * P].rearrange("(m p) g -> p m g", m=2), result[:])
+            result = held.tile([P, 2, n], F32, name=f"result{name}")
+            copy(result[:], acc[:])
+            nc.sync.dma_start(out[:, g0 : g0 + n].rearrange("(m p) g -> p m g", m=2), result[:])
 
+        def round_second(k):
+            turned = held.tile([P, P, 2], BF16, name=f"turned{k}")
+            return round_pair(turned[:], sums[k][1].rearrange("g e p -> g p e"), 1, k)
+
+        waiting = []
+        for k in range(2):
+            sum_corners(gather_chunk(3, k), 3, k)
+            waiting.append(round_second(k))
+        for item in waiting:
+            turn_back(*item)
+        nc.scalar.copy(grouped[3].bitcast(F32).rearrange("p (g u) -> p g u", u=2)[:, :, 0], backs[3][:, 0, :])
+        nc.scalar.copy(
+            grouped[3].rearrange("p (g t) -> p g t", t=PACK)[:, :, 2:4], direct[:].unsqueeze(2).to_broadcast([P, P, 2])
+        )
+
+        third = held.tile([P, PIECE], F32, name="third")
+        gather(third[:], 3, 2 * PIECE)
         nc.vector.quantize_mx(
             out=w_codes[:].bitcast(FP8X4), scales=w_scales[:], in_=w_grouped[:].rearrange("p m t -> p (m t)")
         )
+        reduce_corners(third[:], 2, 0)
         prod = held.tile([P, PIECE], F32, name="last_prod", tag="w_grouped", align_bytes=64)
         halves = [prod[:, h * PIECE // 2 : (h + 1) * PIECE // 2] for h in range(2)]
-        for h in range(2):
-            gather(halves[h], 3, 3 * PIECE + h * PIECE // 2)
-        for h in range(2):
-            reduce_corners(halves[h], 3, h * P // 2)
-        for k in (0, 3, 1):
-            finish(k, *quantize(grouped[k], str(k)))
-        c2, s2 = quantize(grouped[2], "2")
-        result = held.tile([P, 2, P], F32, name="result2")
-        for m, bank in enumerate(("fore2", "back3")):
-            acc = psum.tile([P, P], F32, name=f"acc2_{m}", tag=bank)
-            multiply(acc[:], m, c2, s2)
-            if m == 0:
-                nc.scalar.copy(result[:, m, :], acc[:])
-            else:
-                nc.vector.tensor_copy(result[:, m, :], acc[:])
-        nc.sync.dma_start(out[:, 2 * P : 3 * P].rearrange("(m p) g -> p m g", m=2), result[:])
+        gather(halves[0], 3, 3 * PIECE)
+        finish("0", "fore0", 0, nc.scalar.copy, *quantize(grouped[0], "0"))
+        gather(halves[1], 3, 3 * PIECE + PIECE // 2)
+        finish("2", "fore2", 2 * P, nc.scalar.copy, *quantize(grouped[2], "2"))
+        reduce_corners(halves[0], 3, 0)
+        finish("1", "fore1", P, nc.scalar.copy, *quantize(grouped[1], "1"))
+        reduce_corners(halves[1], 3, P // 2)
+        last = [quantize(grouped[3][:, h * PIECE // 2 : (h + 1) * PIECE // 2], f"3{h}") for h in range(2)]
+        finish("30", "fore3", 3 * P, nc.scalar.copy, *last[0])
+        finish("31", "back3", 3 * P + P // 2, nc.vector.tensor_copy, *last[1])

@@ -11,6 +11,7 @@ U8 = mybir.dt.uint8
 FP8X4 = mybir.dt.float8_e4m3fn_x4
 MULT = mybir.AluOpType.mult
 ADD = mybir.AluOpType.add
+COPY = mybir.ActivationFunctionType.Copy
 
 P = 128
 T = 4096
@@ -23,9 +24,7 @@ PACK = 4
 FLOPS = 2 * D * M * G
 CHUNKS = G // P
 PIECE = P * K
-
-SHARED = 2
-COPY = mybir.ActivationFunctionType.Copy
+FUSED = 3 * PIECE
 
 
 def tile_attend_grid_kernel(tc, xT, w, part, offs, out):
@@ -33,125 +32,138 @@ def tile_attend_grid_kernel(tc, xT, w, part, offs, out):
     x_planes = xT.rearrange("(p t) c -> p t c", t=PACK)
     with ExitStack() as ctx:
         held = ctx.enter_context(tc.tile_pool(name="held", bufs=1))
-        ring = ctx.enter_context(tc.tile_pool(name="ring", bufs=4))
-        wide = ctx.enter_context(tc.tile_pool(name="wide", bufs=3))
+        placed = ctx.enter_context(tc.tile_pool(name="placed", bufs=1))
         psum = ctx.enter_context(tc.psum_pool(name="psum", bufs=1))
 
         offsets = held.tile([P, E // 16], U16, name="offsets")
         nc.sync.dma_start(offsets[:], offs)
-        part_col = held.tile([P, E // P], F32, name="part_col")
-        nc.scalar.dma_start(part_col[:], part[0:1, :].rearrange("o (q i) -> (o q) i", i=E // P))
+        part_col = held.tile([P, FUSED // P], F32, name="part_col", tag="stage0", align_bytes=64)
+        nc.scalar.dma_start(part_col[:], part[0:1, :FUSED].rearrange("o (q i) -> (o q) i", i=FUSED // P))
         part_last = held.tile([P, K], F32, name="part_last")
         nc.scalar.dma_start(part_last[:], part[0:1, 3 * PIECE :].rearrange("o (g j) -> (o g) j", j=K))
         planes = []
         for t in range(PACK):
             plane = held.tile([P, T], F32, name=f"plane{t}")
-            loads = 4 if t == SHARED else 1
-            for h in range(loads):
-                cols = slice(h * T // loads, (h + 1) * T // loads)
-                nc.sync.dma_start(plane[:, cols], x_planes[:, t, cols])
+            nc.sync.dma_start(plane[:], x_planes[:, t, :])
             planes.append(plane)
         w_raw = held.tile([P, PACK, M], F32, name="w_raw", tag="w_raw", align_bytes=64)
         nc.sync.dma_start(w_raw[:], w.rearrange("(p t) m -> p t m", t=PACK))
 
         ident = held.tile([P, P], F32, name="ident")
         make_identity(nc, ident[:])
-        ident_narrow = held.tile([P, P], BF16, name="ident_narrow")
-        make_identity(nc, ident_narrow[:])
 
-        part_rep = held.tile([P, E], F32, name="part_rep")
-        part_view = part_rep[:].rearrange("p (q i) -> p q i", i=E // P)
-        for b in range(4):
-            bank = psum.tile([P, 4, P], F32, name=f"part_bank{b}", tag=f"back{b}")
+        part_rep = held.tile([P, FUSED], F32, name="part_rep", tag="part_rep", align_bytes=64)
+        part_view = part_rep[:].rearrange("p (q i) -> p q i", i=FUSED // P)
+        for b in range(3):
+            bank = psum.tile([P, 4, P], F32, name=f"part_bank{b}", tag=f"bank{b}")
             for i in range(4):
                 col = part_col[:, 4 * b + i : 4 * b + i + 1]
                 nc.tensor.transpose(bank[:, i, :], col.to_broadcast([P, P]), ident[:])
-            src = bank[:].rearrange("p i q -> p q i")
-            dst = part_view[:, :, 4 * b : 4 * b + 4]
-            if b % 2 == 0:
-                nc.vector.tensor_copy(dst, src)
-            else:
-                nc.scalar.copy(dst, src)
+            copy = nc.scalar.copy if b == 0 else nc.vector.tensor_copy
+            copy(part_view[:, :, 4 * b : 4 * b + 4], bank[:].rearrange("p i q -> p q i"))
 
-        first = [psum.tile([P, PACK, P], F32, name=f"first{k}", tag=f"back{k}") for k in range(CHUNKS)]
-        second = [psum.tile([P, 2, P], F32, name=f"second{k}", tag=f"fore{k}") for k in range(CHUNKS - 1)]
-        sums = [(first[k][:, 0:2, :], second[k][:] if k < CHUNKS - 1 else None) for k in range(CHUNKS)]
-        backs = [first[k][:, 2:4, :] for k in range(CHUNKS)]
+        first = [psum.tile([P, PACK, P], F32, name=f"first{k}", tag=f"bank{k}") for k in range(3)]
+        second = [psum.tile([P, PACK, P], F32, name=f"second{k}", tag=f"bank{4 + k}") for k in range(2)]
+        direct = psum.tile([P, PACK, P], F32, name="direct", tag="bank3")
+        backs = [first[k][:, 2:4, :] for k in range(3)]
 
-        w_grouped = held.tile([P, M, PACK], BF16, name="w_grouped", tag="w_grouped", align_bytes=64)
         w_codes = held.tile([P, M], U32, name="w_codes", align_bytes=64)
         w_scales = held.tile([P, M], U8, name="w_scales", align_bytes=64)
         grouped = [
-            held.tile([P, P * PACK], BF16, name=f"grouped{k}", tag=f"grouped{k}", align_bytes=64)[:] for k in range(2)
+            held.tile([P, P * PACK], BF16, name=f"grouped{k}", tag=f"grouped{k}", align_bytes=64)[:] for k in range(CHUNKS)
         ]
+
+        def window(t, e0, n):
+            return planes[t][:].indirect(offsets[:, e0 // 16 : (e0 + n) // 16])
 
         def gather(prod, t, e0):
             n = prod.shape[1]
-            nc.vector.tensor_tensor(
-                prod, planes[t][:].indirect(offsets[:, e0 // 16 : (e0 + n) // 16]), part_rep[:, e0 : e0 + n], MULT
-            )
+            nc.vector.tensor_tensor(prod, window(t, e0, n), part_rep[:, e0 : e0 + n], MULT)
 
-        def sum_corners(corners, t, k):
+        def add_turned(acc, corners):
             for j in range(K):
-                nc.tensor.matmul(
-                    sums[k][t // 2][:, t % 2, :], corners[:, j, :], ident[:], start=(j == 0), stop=(j == K - 1), is_transpose=True
+                nc.tensor.matmul(acc, corners[j], ident[:], start=(j == 0), stop=(j == K - 1), is_transpose=True)
+
+        def gather_and_turn(t, k, prod):
+            gather(prod, t, k * PIECE)
+            acc = first[k][:, t, :] if t < 2 else second[k][:, t - 2, :]
+            add_turned(acc, [prod.rearrange("p (g j) -> p j g", j=K)[:, j, :] for j in range(K)])
+
+        def round_pair(k, u, turned):
+            src = first[k][:, 0:2, :] if u == 0 else second[k][:, 0:2, :]
+            nc.scalar.copy(turned.bitcast(BF16).rearrange("g (p e) -> g p e", e=2), src.rearrange("g e p -> g p e"))
+            nc.tensor.transpose(backs[k][:, u, :], turned, ident[:])
+
+        def words_of(k):
+            return grouped[k].bitcast(F32).rearrange("p (g u) -> p g u", u=2)
+
+        def slots_of(k):
+            return grouped[k].rearrange("p (g t) -> p g t", t=PACK)
+
+        def reduce_corners(prod, t, k, g0):
+            n = prod.shape[1] // K
+            with nc.allow_low_precision(reason="the float32 sum of four products is rounded to bfloat16 once"):
+                nc.vector.tensor_reduce(
+                    slots_of(k)[:, g0 : g0 + n, t], prod.rearrange("p (g j) -> p g j", j=K), mybir.AxisListType.X, ADD
                 )
 
-        def round_pair(turned, src, u, k):
-            nc.scalar.copy(turned, src)
-            return turned, u, k
+        def pick(t, corners, picked):
+            nc.scalar.activation(picked, window(t, 3 * PIECE, PIECE), COPY)
+            pairs = picked.bitcast(F32).rearrange("p (g u) -> p u g", u=2)
+            for u in range(2):
+                nc.tensor.transpose(corners[:, u, :], pairs[:, u, :], ident[:])
+            return corners.rearrange("g u p -> g (u p)").bitcast(BF16).rearrange("g (u p e) -> g u e p", u=2, e=2)
 
-        def turn_back(turned, u, k):
-            nc.tensor.transpose(backs[k][:, u, :], turned.rearrange("g p e -> g (p e)").bitcast(F32), ident[:])
-            if u == 1:
-                words = grouped[k].bitcast(F32).rearrange("p (g u) -> p g u", u=2)
-                nc.scalar.copy(words, backs[k].rearrange("p u g -> p g u"))
+        def weigh(t, corners, weighed):
+            for j in range(K):
+                nc.scalar.activation(weighed[j], corners[:, j // 2, j % 2, :], COPY, scale=part_last[:, j : j + 1])
+            add_turned(direct[:, t, :], weighed)
 
-        def gather_chunk(t, k):
-            prod = ring.tile([P, PIECE], F32, name="prod")
-            gather(prod[:], t, k * PIECE)
-            return prod[:].rearrange("p (g j) -> p j g", j=K)
+        def leave_direct(u):
+            nc.scalar.copy(slots_of(3)[:, :, 2 * u : 2 * u + 2], direct[:, 2 * u : 2 * u + 2, :].rearrange("p t g -> p g t"))
 
-        for t in range(SHARED):
-            for half in range(2):
-                prod = wide.tile([P, 2 * PIECE], F32, name="wide_prod")
-                gather(prod[:], t, half * 2 * PIECE)
-                for c in range(2):
-                    corners = prod[:, c * PIECE : (c + 1) * PIECE].rearrange("p (g j) -> p j g", j=K)
-                    sum_corners(corners, t, 2 * half + c)
+        def stage(t):
+            room = held.tile([P, 4 * PIECE], F32, name=f"room{t}", tag=f"stage{t}", align_bytes=64)
+            prods = [room[:, i * PIECE : (i + 1) * PIECE] for i in range(3)]
+            picked = room[:, 3 * PIECE : 3 * PIECE + PIECE // 2].bitcast(BF16)
+            return prods, picked
 
-        narrow = held.tile([P, T], BF16, name="narrow", tag="narrow")
-        for h in range(4):
-            cols = slice(h * T // 4, (h + 1) * T // 4)
-            nc.scalar.activation(narrow[:, cols], planes[SHARED][:, cols], COPY)
-        for k in (2, 0):
-            sum_corners(gather_chunk(SHARED, k), SHARED, k)
+        def weighed_tile(t):
+            most = held.tile([P, K - 1, P], F32, name=f"weighed{t}", tag=f"stage{t + 1}", align_bytes=64)
+            if t < 2:
+                last = held.tile([P, P], F32, name=f"weighed_last{t}")
+            else:
+                last = placed.tile([P, P], F32, name=f"weighed_last{t}", offset=0, align_bytes=64)
+            return [most[:, j, :] for j in range(K - 1)] + [last[:]]
 
-        picked = held.tile([P, PIECE], BF16, name="picked")
-        nc.scalar.activation(picked[:], narrow[:].indirect(offsets[:, 3 * PIECE // 16 :]), COPY)
-        corners = psum.tile([P, K, P], BF16, name="corners", tag="fore3")
-        for j in range(K):
-            nc.tensor.transpose(corners[:, j, :], picked[:].rearrange("p (g j) -> p j g", j=K)[:, j, :], ident_narrow[:])
-        after_narrow = held.tile([P, 2 * PIECE], F32, name="after_narrow", tag="narrow")
-        gather(after_narrow[:, :PIECE], SHARED, PIECE)
-        sum_corners(after_narrow[:, :PIECE].rearrange("p (g j) -> p j g", j=K), SHARED, 1)
-        weighed = held.tile([P, K, P], F32, name="weighed")
-        for j in range(K):
-            nc.scalar.activation(weighed[:, j, :], corners[:, j, :], COPY, scale=part_last[:, j : j + 1])
-        direct = psum.tile([P, P], F32, name="direct", tag="fore3")
-        for j in range(K):
-            nc.tensor.matmul(direct[:], weighed[:, j, :], ident[:], start=(j == 0), stop=(j == K - 1), is_transpose=True)
+        for t in range(2):
+            prods, picked = stage(t)
+            corners = pick(t, first[0][:, 2:4, :], picked)
+            gather_and_turn(t, 2, prods[0])
+            gather_and_turn(t, 1, prods[1])
+            weigh(t, corners, weighed_tile(t))
+            gather_and_turn(t, 0, prods[2])
+        leave_direct(0)
+        for k in (2, 1):
+            turned = held.tile([P, P], F32, name=f"turned{k}")
+            round_pair(k, 0, turned[:])
+        nc.scalar.copy(words_of(2)[:, :, 0], backs[2][:, 0, :])
 
-        early = after_narrow[:, PIECE:].bitcast(BF16).rearrange("g (k p e) -> g k p e", k=CHUNKS, e=2)
-        for k in (2, 3, 0, 1):
-            turn_back(*round_pair(early[:, k], sums[k][0].rearrange("g e p -> g p e"), 0, k))
-        doubled = held.tile([P, P, 2], BF16, name="doubled")
-        nc.scalar.copy(doubled[:], sums[2][1][:, 0, :].unsqueeze(2).to_broadcast([P, P, 2]))
-        nc.tensor.transpose(backs[2][:, 1, :], doubled[:].rearrange("g p e -> g (p e)").bitcast(F32), ident[:])
-        nc.scalar.copy(w_grouped[:], w_raw[:].rearrange("p t m -> p m t"))
-        after_w = held.tile([P, 2 * P * PACK], BF16, name="after_w", tag="w_raw", align_bytes=64)
-        grouped.extend([after_w[:, : P * PACK], after_w[:, P * PACK :]])
-        nc.scalar.copy(grouped[2].bitcast(F32).rearrange("p (g u) -> p g u", u=2), backs[2].rearrange("p u g -> p g u"))
+        prods, picked = stage(2)
+        corners = pick(2, second[0][:, 2:4, :], picked)
+        gather_and_turn(2, 1, prods[0])
+        gather(prods[1], 2, 2 * PIECE)
+        doubled = held.tile([P, P], F32, name="doubled", tag="doubled")
+        nc.scalar.copy(
+            doubled[:].bitcast(BF16).rearrange("g (p e) -> g p e", e=2), second[1][:, 0, :].unsqueeze(2).to_broadcast([P, P, 2])
+        )
+        nc.tensor.transpose(backs[1][:, 1, :], doubled[:], ident[:])
+        weigh(2, corners, weighed_tile(2))
+        nc.scalar.copy(words_of(1), backs[1].rearrange("p u g -> p g u"))
+        turned = held.tile([P, P], F32, name="turned0", tag="doubled")
+        round_pair(0, 0, turned[:])
+        gather_and_turn(2, 0, prods[2])
+        reduce_corners(prods[1], 2, 2, 0)
 
         def quantize(flat, name, codes=None):
             n = flat.shape[1] // PACK
@@ -161,67 +173,56 @@ def tile_attend_grid_kernel(tc, xT, w, part, offs, out):
             nc.vector.quantize_mx(out=codes.bitcast(FP8X4), scales=scales[:], in_=flat)
             return codes, scales
 
-        def multiply(acc, m, codes, scales):
-            cols = slice(m * P, (m + 1) * P)
-            nc.tensor.matmul_mx(
-                out=acc,
-                lhsT=w_codes[:, cols].bitcast(FP8X4),
-                lhsT_scale=w_scales[:, cols],
-                rhs=codes.bitcast(FP8X4),
-                rhs_scale=scales[:],
-                start=True,
-                stop=True,
-            )
-
-        def reduce_corners(prod, k, g0):
-            n = prod.shape[1] // K
-            with nc.allow_low_precision(reason="the float32 sum of four products is rounded to bfloat16 once"):
-                nc.vector.tensor_reduce(
-                    grouped[k].rearrange("p (g t) -> p g t", t=PACK)[:, g0 : g0 + n, 3],
-                    prod[:].rearrange("p (g j) -> p g j", j=K),
-                    mybir.AxisListType.X,
-                    ADD,
-                )
-
         def finish(name, bank, g0, copy, codes, scales):
             n = codes.shape[1]
             acc = psum.tile([P, 2, n], F32, name=f"acc{name}", tag=bank)
             for m in range(2):
-                multiply(acc[:, m, :], m, codes, scales)
+                cols = slice(m * P, (m + 1) * P)
+                nc.tensor.matmul_mx(
+                    out=acc[:, m, :],
+                    lhsT=w_codes[:, cols].bitcast(FP8X4),
+                    lhsT_scale=w_scales[:, cols],
+                    rhs=codes.bitcast(FP8X4),
+                    rhs_scale=scales[:],
+                    start=True,
+                    stop=True,
+                )
             result = held.tile([P, 2, n], F32, name=f"result{name}")
             copy(result[:], acc[:])
             nc.sync.dma_start(out[:, g0 : g0 + n].rearrange("(m p) g -> p m g", m=2), result[:])
 
-        def round_second(k):
-            turned = held.tile([P, P, 2], BF16, name=f"turned{k}")
-            return round_pair(turned[:], sums[k][1].rearrange("g e p -> g p e"), 1, k)
+        half = PIECE // 2
+        last_corners = psum.tile([P, 2, P], F32, name="last_corners", tag="bank6")
+        prods, picked = stage(3)
+        corners = pick(3, last_corners[:], picked)
+        w_grouped = placed.tile([P, M * PACK], BF16, name="w_grouped", offset=0, align_bytes=64)[:]
+        nc.scalar.copy(w_grouped.rearrange("p (m t) -> p m t", t=PACK), w_raw[:].rearrange("p t m -> p m t"))
+        gather_and_turn(3, 0, prods[0])
+        after_w = held.tile([P, K + 1, P], F32, name="after_w", tag="w_raw", align_bytes=64)
+        weigh(3, corners, [after_w[:, j, :] for j in range(K)])
+        round_pair(0, 1, after_w[:, K, :])
+        leave_direct(1)
+        nc.scalar.copy(words_of(0), backs[0].rearrange("p u g -> p g u"))
 
-        waiting = []
-        for k in range(2):
-            sum_corners(gather_chunk(3, k), 3, k)
-            waiting.append(round_second(k))
-        for item in waiting:
-            turn_back(*item)
-        nc.scalar.copy(grouped[3].bitcast(F32).rearrange("p (g u) -> p g u", u=2)[:, :, 0], backs[3][:, 0, :])
-        nc.scalar.copy(
-            grouped[3].rearrange("p (g t) -> p g t", t=PACK)[:, :, 2:4], direct[:].unsqueeze(2).to_broadcast([P, P, 2])
-        )
-
-        third = held.tile([P, PIECE], F32, name="third")
-        gather(third[:], 3, 2 * PIECE)
+        prod = prods[1]
+        for h in range(2):
+            gather(prod[:, h * half : (h + 1) * half], 3, PIECE + h * half)
+        for h in range(2):
+            reduce_corners(prod[:, h * half : (h + 1) * half], 3, 1, h * P // 2)
         nc.vector.quantize_mx(
-            out=w_codes[:].bitcast(FP8X4), scales=w_scales[:], in_=w_grouped[:].rearrange("p m t -> p (m t)")
+            out=w_codes[:].bitcast(FP8X4), scales=w_scales[:], in_=w_grouped
         )
-        reduce_corners(third[:], 2, 0)
-        prod = held.tile([P, PIECE], F32, name="last_prod", tag="w_grouped", align_bytes=64)
-        halves = [prod[:, h * PIECE // 2 : (h + 1) * PIECE // 2] for h in range(2)]
-        gather(halves[0], 3, 3 * PIECE)
-        finish("0", "fore0", 0, nc.scalar.copy, *quantize(grouped[0], "0"))
-        gather(halves[1], 3, 3 * PIECE + PIECE // 2)
-        finish("2", "fore2", 2 * P, nc.scalar.copy, *quantize(grouped[2], "2"))
-        reduce_corners(halves[0], 3, 0)
-        finish("1", "fore1", P, nc.scalar.copy, *quantize(grouped[1], "1"))
-        reduce_corners(halves[1], 3, P // 2)
-        last = [quantize(grouped[3][:, h * PIECE // 2 : (h + 1) * PIECE // 2], f"3{h}") for h in range(2)]
-        finish("30", "fore3", 3 * P, nc.scalar.copy, *last[0])
-        finish("31", "back3", 3 * P + P // 2, nc.vector.tensor_copy, *last[1])
+        third = placed.tile([P, half], F32, name="third", offset=0, align_bytes=64)
+        gather(third[:], 3, 2 * PIECE)
+        after_wq = placed.tile([P, P], U32, name="after_wq", offset=4 * half, align_bytes=64)
+        finish("1", "bank0", P, nc.scalar.copy, *quantize(grouped[1], "1", after_wq[:]))
+        reduce_corners(third[:], 3, 2, 0)
+        finish("3", "bank7", 3 * P, nc.scalar.copy, *quantize(grouped[3], "3"))
+        fourth = held.tile([P, half], F32, name="fourth", tag="grouped3", align_bytes=64)
+        gather(fourth[:], 3, 2 * PIECE + half)
+        after_part = held.tile([P, P], U32, name="after_part", tag="part_rep", align_bytes=64)
+        finish("0", "bank1", 0, nc.scalar.copy, *quantize(grouped[0], "0", after_part[:]))
+        reduce_corners(fourth[:], 3, 2, P // 2)
+        after_0 = held.tile([P, P // 2], U32, name="after_0", tag="grouped0", align_bytes=64)
+        finish("20", "bank5", 2 * P, nc.scalar.copy, *quantize(grouped[2][:, :half], "20", after_0[:]))
+        finish("21", "bank2", 2 * P + P // 2, nc.vector.tensor_copy, *quantize(grouped[2][:, half:], "21"))

@@ -62,10 +62,10 @@ def tile_attend_grid_kernel(tc, xT, w, part, offs, out):
             copy = nc.scalar.copy if b == 0 else nc.vector.tensor_copy
             copy(part_view[:, :, 4 * b : 4 * b + 4], bank[:].rearrange("p i q -> p q i"))
 
-        first = [psum.tile([P, PACK, P], F32, name=f"first{k}", tag=f"bank{k}") for k in range(3)]
-        second = [psum.tile([P, PACK, P], F32, name=f"second{k}", tag=f"bank{4 + k}") for k in range(2)]
+        first = [psum.tile([P, PACK, P], F32, name=f"first{k}", tag=f"bank{k}") for k in range(2)]
+        second = psum.tile([P, PACK, P], F32, name="second", tag="bank4")
         direct = psum.tile([P, PACK, P], F32, name="direct", tag="bank3")
-        backs = [first[k][:, 2:4, :] for k in range(3)]
+        backs = [first[k][:, 2:4, :] for k in range(2)]
 
         w_codes = held.tile([P, M], U32, name="w_codes", align_bytes=64)
         w_scales = held.tile([P, M], U8, name="w_scales", align_bytes=64)
@@ -86,11 +86,11 @@ def tile_attend_grid_kernel(tc, xT, w, part, offs, out):
 
         def gather_and_turn(t, k, prod):
             gather(prod, t, k * PIECE)
-            acc = first[k][:, t, :] if t < 2 else second[k][:, t - 2, :]
+            acc = first[k][:, t, :] if t < 2 else second[:, t - 2, :]
             add_turned(acc, [prod.rearrange("p (g j) -> p j g", j=K)[:, j, :] for j in range(K)])
 
         def round_pair(k, u, turned):
-            src = first[k][:, 0:2, :] if u == 0 else second[k][:, 0:2, :]
+            src = first[k][:, 0:2, :] if u == 0 else second[:, 0:2, :]
             nc.scalar.copy(turned.bitcast(BF16).rearrange("g (p e) -> g p e", e=2), src.rearrange("g e p -> g p e"))
             nc.tensor.transpose(backs[k][:, u, :], turned, ident[:])
 
@@ -130,40 +130,40 @@ def tile_attend_grid_kernel(tc, xT, w, part, offs, out):
 
         def weighed_tile(t):
             most = held.tile([P, K - 1, P], F32, name=f"weighed{t}", tag=f"stage{t + 1}", align_bytes=64)
-            if t < 2:
-                last = held.tile([P, P], F32, name=f"weighed_last{t}")
-            else:
-                last = placed.tile([P, P], F32, name=f"weighed_last{t}", offset=0, align_bytes=64)
+            last = placed.tile([P, P], F32, name=f"weighed_last{t}", offset=(16 * PIECE, 8 * PIECE, 0)[t], align_bytes=64)
             return [most[:, j, :] for j in range(K - 1)] + [last[:]]
 
         for t in range(2):
             prods, picked = stage(t)
             corners = pick(t, first[0][:, 2:4, :], picked)
-            gather_and_turn(t, 2, prods[0])
-            gather_and_turn(t, 1, prods[1])
+            gather_and_turn(t, 1, prods[0])
+            gather(prods[1], t, 2 * PIECE)
+            if t == 1:
+                turned = held.tile([P, P], F32, name="turned1")
+                round_pair(1, 0, turned[:])
             weigh(t, corners, weighed_tile(t))
             gather_and_turn(t, 0, prods[2])
+            reduce_corners(prods[1], t, 2, 0)
+        nc.scalar.copy(words_of(1)[:, :, 0], backs[1][:, 0, :])
         leave_direct(0)
-        for k in (2, 1):
-            turned = held.tile([P, P], F32, name=f"turned{k}")
-            round_pair(k, 0, turned[:])
-        nc.scalar.copy(words_of(2)[:, :, 0], backs[2][:, 0, :])
 
+        half = PIECE // 2
         prods, picked = stage(2)
-        corners = pick(2, second[0][:, 2:4, :], picked)
-        gather_and_turn(2, 1, prods[0])
+        third_corners = psum.tile([P, 2, P], F32, name="third_corners", tag="bank5")
+        corners = pick(2, third_corners[:], picked)
+        plain = placed.tile([P, PIECE], F32, name="plain", offset=8 * PIECE, align_bytes=64)
+        nc.scalar.activation(plain[:], window(2, PIECE, PIECE), COPY)
         gather(prods[1], 2, 2 * PIECE)
-        doubled = held.tile([P, P], F32, name="doubled", tag="doubled")
-        nc.scalar.copy(
-            doubled[:].bitcast(BF16).rearrange("g (p e) -> g p e", e=2), second[1][:, 0, :].unsqueeze(2).to_broadcast([P, P, 2])
-        )
-        nc.tensor.transpose(backs[1][:, 1, :], doubled[:], ident[:])
-        weigh(2, corners, weighed_tile(2))
-        nc.scalar.copy(words_of(1), backs[1].rearrange("p u g -> p g u"))
-        turned = held.tile([P, P], F32, name="turned0", tag="doubled")
-        round_pair(0, 0, turned[:])
         gather_and_turn(2, 0, prods[2])
         reduce_corners(prods[1], 2, 2, 0)
+        for h in range(2):
+            cols = slice(h * half, (h + 1) * half)
+            nc.vector.tensor_tensor(prods[0][:, cols], plain[:, cols], part_rep[:, PIECE + h * half : PIECE + (h + 1) * half], MULT)
+        for h in range(2):
+            reduce_corners(prods[0][:, h * half : (h + 1) * half], 2, 1, h * P // 2)
+        weigh(2, corners, weighed_tile(2))
+        turned = placed.tile([P, P], F32, name="turned0", offset=8 * PIECE, align_bytes=64)
+        round_pair(0, 0, turned[:])
 
         def quantize(flat, name, codes=None):
             n = flat.shape[1] // PACK
@@ -191,7 +191,6 @@ def tile_attend_grid_kernel(tc, xT, w, part, offs, out):
             copy(result[:], acc[:])
             nc.sync.dma_start(out[:, g0 : g0 + n].rearrange("(m p) g -> p m g", m=2), result[:])
 
-        half = PIECE // 2
         last_corners = psum.tile([P, 2, P], F32, name="last_corners", tag="bank6")
         prods, picked = stage(3)
         corners = pick(3, last_corners[:], picked)
@@ -215,7 +214,7 @@ def tile_attend_grid_kernel(tc, xT, w, part, offs, out):
         third = placed.tile([P, half], F32, name="third", offset=0, align_bytes=64)
         gather(third[:], 3, 2 * PIECE)
         after_wq = placed.tile([P, P], U32, name="after_wq", offset=4 * half, align_bytes=64)
-        finish("1", "bank0", P, nc.scalar.copy, *quantize(grouped[1], "1", after_wq[:]))
+        finish("1", "bank3", P, nc.scalar.copy, *quantize(grouped[1], "1", after_wq[:]))
         reduce_corners(third[:], 3, 2, 0)
         finish("3", "bank7", 3 * P, nc.scalar.copy, *quantize(grouped[3], "3"))
         fourth = held.tile([P, half], F32, name="fourth", tag="grouped3", align_bytes=64)

@@ -25,6 +25,7 @@ FLOPS = 2 * D * M * G
 CHUNKS = G // P
 PIECE = P * K
 FUSED = 3 * PIECE
+W_AT = 20 * PIECE
 
 
 def tile_attend_grid_kernel(tc, xT, w, part, offs, out):
@@ -46,7 +47,7 @@ def tile_attend_grid_kernel(tc, xT, w, part, offs, out):
             plane = held.tile([P, T], F32, name=f"plane{t}")
             nc.sync.dma_start(plane[:], x_planes[:, t, :])
             planes.append(plane)
-        w_raw = held.tile([P, PACK, M], F32, name="w_raw", tag="w_raw", align_bytes=64)
+        w_raw = placed.tile([P, PACK, M], F32, name="w_raw", offset=W_AT, align_bytes=64)
         nc.sync.dma_start(w_raw[:], w.rearrange("(p t) m -> p t m", t=PACK))
 
         ident = held.tile([P, P], F32, name="ident")
@@ -61,6 +62,13 @@ def tile_attend_grid_kernel(tc, xT, w, part, offs, out):
                 nc.tensor.transpose(bank[:, i, :], col.to_broadcast([P, P]), ident[:])
             copy = nc.scalar.copy if b == 0 else nc.vector.tensor_copy
             copy(part_view[:, :, 4 * b : 4 * b + 4], bank[:].rearrange("p i q -> p q i"))
+
+        half = PIECE // 2
+        part_half = held.tile([P, 2], F32, name="part_half")
+        bank = psum.tile([P, 2, P], F32, name="half_bank", tag="bank3")
+        for e in range(2):
+            nc.tensor.transpose(bank[:, e, :], part_rep[:, FUSED - half + e : FUSED : 2], ident[:])
+        nc.vector.tensor_copy(part_half[:], bank[:, :, 0])
 
         first = [psum.tile([P, PACK, P], F32, name=f"first{k}", tag=f"bank{k}") for k in range(2)]
         second = psum.tile([P, PACK, P], F32, name="second", tag="bank4")
@@ -81,8 +89,8 @@ def tile_attend_grid_kernel(tc, xT, w, part, offs, out):
             nc.vector.tensor_tensor(prod, window(t, e0, n), part_rep[:, e0 : e0 + n], MULT)
 
         def add_turned(acc, corners):
-            for j in range(K):
-                nc.tensor.matmul(acc, corners[j], ident[:], start=(j == 0), stop=(j == K - 1), is_transpose=True)
+            for j, corner in enumerate(corners):
+                nc.tensor.matmul(acc, corner, ident[:], start=(j == 0), stop=(j == len(corners) - 1), is_transpose=True)
 
         def gather_and_turn(t, k, prod):
             gather(prod, t, k * PIECE)
@@ -101,10 +109,10 @@ def tile_attend_grid_kernel(tc, xT, w, part, offs, out):
             return grouped[k].rearrange("p (g t) -> p g t", t=PACK)
 
         def reduce_corners(prod, t, k, g0):
-            n = prod.shape[1] // K
+            n = P // 2 if prod.shape[1] < PIECE else P
             with nc.allow_low_precision(reason="the float32 sum of four products is rounded to bfloat16 once"):
                 nc.vector.tensor_reduce(
-                    slots_of(k)[:, g0 : g0 + n, t], prod.rearrange("p (g j) -> p g j", j=K), mybir.AxisListType.X, ADD
+                    slots_of(k)[:, g0 : g0 + n, t], prod.rearrange("p (g j) -> p g j", g=n), mybir.AxisListType.X, ADD
                 )
 
         def pick(t, corners, picked):
@@ -147,7 +155,6 @@ def tile_attend_grid_kernel(tc, xT, w, part, offs, out):
         nc.scalar.copy(words_of(1)[:, :, 0], backs[1][:, 0, :])
         leave_direct(0)
 
-        half = PIECE // 2
         prods, picked = stage(2)
         third_corners = psum.tile([P, 2, P], F32, name="third_corners", tag="bank5")
         corners = pick(2, third_corners[:], picked)
@@ -173,7 +180,7 @@ def tile_attend_grid_kernel(tc, xT, w, part, offs, out):
             nc.vector.quantize_mx(out=codes.bitcast(FP8X4), scales=scales[:], in_=flat)
             return codes, scales
 
-        def finish(name, bank, g0, copy, codes, scales):
+        def finish(name, bank, g0, copy, codes, scales, tag=None):
             n = codes.shape[1]
             acc = psum.tile([P, 2, n], F32, name=f"acc{name}", tag=bank)
             for m in range(2):
@@ -187,7 +194,7 @@ def tile_attend_grid_kernel(tc, xT, w, part, offs, out):
                     start=True,
                     stop=True,
                 )
-            result = held.tile([P, 2, n], F32, name=f"result{name}")
+            result = held.tile([P, 2, n], F32, name=f"result{name}", tag=tag or f"result{name}", align_bytes=64)
             copy(result[:], acc[:])
             nc.sync.dma_start(out[:, g0 : g0 + n].rearrange("(m p) g -> p m g", m=2), result[:])
 
@@ -197,9 +204,19 @@ def tile_attend_grid_kernel(tc, xT, w, part, offs, out):
         w_grouped = placed.tile([P, M * PACK], BF16, name="w_grouped", offset=0, align_bytes=64)[:]
         nc.scalar.copy(w_grouped.rearrange("p (m t) -> p m t", t=PACK), w_raw[:].rearrange("p t m -> p m t"))
         gather_and_turn(3, 0, prods[0])
-        after_w = held.tile([P, K + 1, P], F32, name="after_w", tag="w_raw", align_bytes=64)
+        after_w = placed.tile([P, K + 1, P], F32, name="after_w", offset=W_AT, align_bytes=64)
+        picked_half = placed.tile([P, half], BF16, name="picked_half", offset=W_AT + 5 * PIECE, align_bytes=64)
+        weighed_half = placed.tile([P, 2, P], F32, name="weighed_half", offset=W_AT + 6 * PIECE, align_bytes=64)
+        nc.scalar.activation(picked_half[:], window(3, FUSED - half, half), COPY)
+        half_corners = psum.tile([P, P], F32, name="half_corners", tag="bank5")
+        nc.tensor.transpose(half_corners[:], picked_half[:].bitcast(F32), ident[:])
         weigh(3, corners, [after_w[:, j, :] for j in range(K)])
         round_pair(0, 1, after_w[:, K, :])
+        half_sums = psum.tile([P, P], F32, name="half_sums", tag="bank2")
+        for e in range(2):
+            pairs = half_corners[:].bitcast(BF16).rearrange("g (p e) -> g e p", e=2)
+            nc.scalar.activation(weighed_half[:, e, :], pairs[:, e, :], COPY, scale=part_half[:, e : e + 1])
+        add_turned(half_sums[:], [weighed_half[:, e, :] for e in range(2)])
         leave_direct(1)
         nc.scalar.copy(words_of(0), backs[0].rearrange("p u g -> p g u"))
 
@@ -216,12 +233,10 @@ def tile_attend_grid_kernel(tc, xT, w, part, offs, out):
         after_wq = placed.tile([P, P], U32, name="after_wq", offset=4 * half, align_bytes=64)
         finish("1", "bank3", P, nc.scalar.copy, *quantize(grouped[1], "1", after_wq[:]))
         reduce_corners(third[:], 3, 2, 0)
-        finish("3", "bank7", 3 * P, nc.scalar.copy, *quantize(grouped[3], "3"))
-        fourth = held.tile([P, half], F32, name="fourth", tag="grouped3", align_bytes=64)
-        gather(fourth[:], 3, 2 * PIECE + half)
-        after_part = held.tile([P, P], U32, name="after_part", tag="part_rep", align_bytes=64)
-        finish("0", "bank1", 0, nc.scalar.copy, *quantize(grouped[0], "0", after_part[:]))
-        reduce_corners(fourth[:], 3, 2, P // 2)
-        after_0 = held.tile([P, P // 2], U32, name="after_0", tag="grouped0", align_bytes=64)
-        finish("20", "bank5", 2 * P, nc.scalar.copy, *quantize(grouped[2][:, :half], "20", after_0[:]))
-        finish("21", "bank2", 2 * P + P // 2, nc.vector.tensor_copy, *quantize(grouped[2][:, half:], "21"))
+        finish("20", "bank0", 2 * P, nc.scalar.copy, *quantize(grouped[2][:, :half], "20"))
+        packed3 = quantize(grouped[3], "3")
+        reduce_corners(half_sums[:], 3, 2, P // 2)
+        finish("0", "bank1", 0, nc.scalar.copy, *quantize(grouped[0], "0"))
+        packed21 = quantize(grouped[2][:, half:], "21")
+        finish("3", "bank7", 3 * P, nc.vector.tensor_copy, *packed3, tag="grouped0")
+        finish("21", "bank4", 2 * P + P // 2, nc.vector.tensor_copy, *packed21)

@@ -194,7 +194,10 @@ def tile_attend_grid_kernel(tc, xT, w, part, offs, out):
                     start=True,
                     stop=True,
                 )
-            result = held.tile([P, 2, n], F32, name=f"result{name}", tag=tag or f"result{name}", align_bytes=64)
+            if name == "1":
+                result = placed.tile([P, 2, n], F32, name="result1", offset=W_AT + 3 * PIECE, align_bytes=64)
+            else:
+                result = held.tile([P, 2, n], F32, name=f"result{name}", tag=tag or f"result{name}", align_bytes=64)
             copy(result[:], acc[:])
             nc.sync.dma_start(out[:, g0 : g0 + n].rearrange("(m p) g -> p m g", m=2), result[:])
 
@@ -204,14 +207,15 @@ def tile_attend_grid_kernel(tc, xT, w, part, offs, out):
         w_grouped = placed.tile([P, M * PACK], BF16, name="w_grouped", offset=0, align_bytes=64)[:]
         nc.scalar.copy(w_grouped.rearrange("p (m t) -> p m t", t=PACK), w_raw[:].rearrange("p t m -> p m t"))
         gather_and_turn(3, 0, prods[0])
-        after_w = placed.tile([P, K + 1, P], F32, name="after_w", offset=W_AT, align_bytes=64)
+        after_w = placed.tile([P, K, P], F32, name="after_w", offset=W_AT, align_bytes=64)
+        last_turned = placed.tile([P, P], F32, name="last_turned", offset=W_AT + 4 * PIECE, align_bytes=64)
         picked_half = placed.tile([P, half], BF16, name="picked_half", offset=W_AT + 5 * PIECE, align_bytes=64)
         weighed_half = placed.tile([P, 2, P], F32, name="weighed_half", offset=W_AT + 6 * PIECE, align_bytes=64)
         nc.scalar.activation(picked_half[:], window(3, FUSED - half, half), COPY)
         half_corners = psum.tile([P, P], F32, name="half_corners", tag="bank5")
         nc.tensor.transpose(half_corners[:], picked_half[:].bitcast(F32), ident[:])
         weigh(3, corners, [after_w[:, j, :] for j in range(K)])
-        round_pair(0, 1, after_w[:, K, :])
+        round_pair(0, 1, last_turned[:])
         half_sums = psum.tile([P, P], F32, name="half_sums", tag="bank2")
         for e in range(2):
             pairs = half_corners[:].bitcast(BF16).rearrange("g (p e) -> g e p", e=2)
@@ -231,12 +235,13 @@ def tile_attend_grid_kernel(tc, xT, w, part, offs, out):
         third = placed.tile([P, half], F32, name="third", offset=0, align_bytes=64)
         gather(third[:], 3, 2 * PIECE)
         after_wq = placed.tile([P, P], U32, name="after_wq", offset=4 * half, align_bytes=64)
-        finish("1", "bank3", P, nc.scalar.copy, *quantize(grouped[1], "1", after_wq[:]))
+        finish("1", "bank6", P, nc.scalar.copy, *quantize(grouped[1], "1", after_wq[:]))
         reduce_corners(third[:], 3, 2, 0)
-        finish("20", "bank0", 2 * P, nc.scalar.copy, *quantize(grouped[2][:, :half], "20"))
-        packed3 = quantize(grouped[3], "3")
+        packed20 = quantize(grouped[2][:, :half], "20")
+        finish("3", "bank7", 3 * P, nc.scalar.copy, *quantize(grouped[3], "3"))
         reduce_corners(half_sums[:], 3, 2, P // 2)
-        finish("0", "bank1", 0, nc.scalar.copy, *quantize(grouped[0], "0"))
+        packed0 = quantize(grouped[0], "0")
         packed21 = quantize(grouped[2][:, half:], "21")
-        finish("3", "bank7", 3 * P, nc.vector.tensor_copy, *packed3, tag="grouped0")
-        finish("21", "bank4", 2 * P + P // 2, nc.vector.tensor_copy, *packed21)
+        finish("20", "bank5", 2 * P, nc.vector.tensor_copy, *packed20, tag="grouped0")
+        finish("0", "bank1", 0, nc.vector.tensor_copy, *packed0)
+        finish("21", "bank4", 2 * P + P // 2, nc.scalar.copy, *packed21)

@@ -205,7 +205,9 @@ def tile_attend_grid_kernel(tc, xT, w, part, offs, out):
         prods, picked = stage(3)
         corners = pick(3, last_corners[:], picked)
         w_grouped = placed.tile([P, M * PACK], BF16, name="w_grouped", offset=0, align_bytes=64)[:]
-        nc.scalar.copy(w_grouped.rearrange("p (m t) -> p m t", t=PACK), w_raw[:].rearrange("p t m -> p m t"))
+        nc.scalar.copy(
+            w_grouped.rearrange("p (c i t) -> p c t i", i=4, t=PACK), w_raw[:].rearrange("p t (c i) -> p c t i", i=4)
+        )
         gather_and_turn(3, 0, prods[0])
         after_w = placed.tile([P, K, P], F32, name="after_w", offset=W_AT, align_bytes=64)
         last_turned = placed.tile([P, P], F32, name="last_turned", offset=W_AT + 4 * PIECE, align_bytes=64)

@@ -22,10 +22,10 @@ K = 4
 E = G * K
 PACK = 4
 FLOPS = 2 * D * M * G
-CHUNKS = G // P
 PIECE = P * K
-FUSED = 3 * PIECE
-W_AT = 20 * PIECE
+HALF = PIECE // 2
+SPREAD = 3 * PIECE
+ROW_ALIGN = 256
 
 
 def tile_attend_grid_kernel(tc, xT, w, part, offs, out):
@@ -33,53 +33,48 @@ def tile_attend_grid_kernel(tc, xT, w, part, offs, out):
     x_planes = xT.rearrange("(p t) c -> p t c", t=PACK)
     with ExitStack() as ctx:
         held = ctx.enter_context(tc.tile_pool(name="held", bufs=1))
-        placed = ctx.enter_context(tc.tile_pool(name="placed", bufs=1))
         psum = ctx.enter_context(tc.psum_pool(name="psum", bufs=1))
 
         offsets = held.tile([P, E // 16], U16, name="offsets")
         nc.sync.dma_start(offsets[:], offs)
-        part_col = held.tile([P, FUSED // P], F32, name="part_col", tag="stage0", align_bytes=64)
-        nc.scalar.dma_start(part_col[:], part[0:1, :FUSED].rearrange("o (q i) -> (o q) i", i=FUSED // P))
+        part_col = held.tile([P, SPREAD // P], F32, name="part_col", tag="stage0", align_bytes=64)
+        nc.scalar.dma_start(part_col[:], part[0:1, :SPREAD].rearrange("o (q i) -> (o q) i", i=SPREAD // P))
         part_last = held.tile([P, K], F32, name="part_last")
-        nc.scalar.dma_start(part_last[:], part[0:1, 3 * PIECE :].rearrange("o (g j) -> (o g) j", j=K))
+        nc.scalar.dma_start(part_last[:], part[0:1, SPREAD:].rearrange("o (g j) -> (o g) j", j=K))
         planes = []
         for t in range(PACK):
-            plane = held.tile([P, T], F32, name=f"plane{t}")
+            plane = held.tile([P, T], F32, name=f"plane{t}", align_bytes=ROW_ALIGN)
             nc.sync.dma_start(plane[:], x_planes[:, t, :])
             planes.append(plane)
-        w_raw = placed.tile([P, PACK, M], F32, name="w_raw", offset=W_AT, align_bytes=64)
+        w_raw = held.tile([P, PACK, M], F32, name="w_raw", align_bytes=ROW_ALIGN)
         nc.sync.dma_start(w_raw[:], w.rearrange("(p t) m -> p t m", t=PACK))
 
         ident = held.tile([P, P], F32, name="ident")
         make_identity(nc, ident[:])
 
-        part_rep = held.tile([P, FUSED], F32, name="part_rep", tag="part_rep", align_bytes=64)
-        part_view = part_rep[:].rearrange("p (q i) -> p q i", i=FUSED // P)
-        for b in range(3):
-            bank = psum.tile([P, 4, P], F32, name=f"part_bank{b}", tag=f"bank{b}")
+        part_rep = held.tile([P, SPREAD], F32, name="part_rep", align_bytes=64)
+        part_view = part_rep[:].rearrange("p (q i) -> p q i", i=SPREAD // P)
+        for b, tag in enumerate(("sums01", "sums23", "backs")):
+            bank = psum.tile([P, 4, P], F32, name=f"part_bank{b}", tag=tag)
             for i in range(4):
                 col = part_col[:, 4 * b + i : 4 * b + i + 1]
                 nc.tensor.transpose(bank[:, i, :], col.to_broadcast([P, P]), ident[:])
             copy = nc.scalar.copy if b == 0 else nc.vector.tensor_copy
             copy(part_view[:, :, 4 * b : 4 * b + 4], bank[:].rearrange("p i q -> p q i"))
 
-        half = PIECE // 2
         part_half = held.tile([P, 2], F32, name="part_half")
-        bank = psum.tile([P, 2, P], F32, name="half_bank", tag="bank3")
+        bank = psum.tile([P, 2, P], F32, name="half_bank", tag="direct")
         for e in range(2):
-            nc.tensor.transpose(bank[:, e, :], part_rep[:, FUSED - half + e : FUSED : 2], ident[:])
+            nc.tensor.transpose(bank[:, e, :], part_rep[:, SPREAD - HALF + e : SPREAD : 2], ident[:])
         nc.vector.tensor_copy(part_half[:], bank[:, :, 0])
 
-        first = [psum.tile([P, PACK, P], F32, name=f"first{k}", tag=f"bank{k}") for k in range(2)]
-        second = psum.tile([P, PACK, P], F32, name="second", tag="bank4")
-        direct = psum.tile([P, PACK, P], F32, name="direct", tag="bank3")
-        backs = [first[k][:, 2:4, :] for k in range(2)]
+        sums = [psum.tile([P, 2, P], F32, name=tag, tag=tag) for tag in ("sums01", "sums23")]
+        backs = psum.tile([P, 2, P], F32, name="backs", tag="backs")
+        direct = psum.tile([P, PACK, P], F32, name="direct", tag="direct")
+        grouped = [held.tile([P, P * PACK], BF16, name=f"grouped{k}", align_bytes=64)[:] for k in range(G // P)]
 
-        w_codes = held.tile([P, M], U32, name="w_codes", align_bytes=64)
-        w_scales = held.tile([P, M], U8, name="w_scales", align_bytes=64)
-        grouped = [
-            held.tile([P, P * PACK], BF16, name=f"grouped{k}", tag=f"grouped{k}", align_bytes=64)[:] for k in range(CHUNKS)
-        ]
+        def slots_of(k):
+            return grouped[k].rearrange("p (g t) -> p g t", t=PACK)
 
         def window(t, e0, n):
             return planes[t][:].indirect(offsets[:, e0 // 16 : (e0 + n) // 16])
@@ -88,162 +83,146 @@ def tile_attend_grid_kernel(tc, xT, w, part, offs, out):
             n = prod.shape[1]
             nc.vector.tensor_tensor(prod, window(t, e0, n), part_rep[:, e0 : e0 + n], MULT)
 
-        def add_turned(acc, corners):
-            for j, corner in enumerate(corners):
-                nc.tensor.matmul(acc, corner, ident[:], start=(j == 0), stop=(j == len(corners) - 1), is_transpose=True)
+        def add_turned(acc, tiles):
+            for j, tile in enumerate(tiles):
+                nc.tensor.matmul(acc, tile, ident[:], start=(j == 0), stop=(j == len(tiles) - 1), is_transpose=True)
 
-        def gather_and_turn(t, k, prod):
-            gather(prod, t, k * PIECE)
-            acc = first[k][:, t, :] if t < 2 else second[:, t - 2, :]
-            add_turned(acc, [prod.rearrange("p (g j) -> p j g", j=K)[:, j, :] for j in range(K)])
-
-        def round_pair(k, u, turned):
-            src = first[k][:, 0:2, :] if u == 0 else second[:, 0:2, :]
-            nc.scalar.copy(turned.bitcast(BF16).rearrange("g (p e) -> g p e", e=2), src.rearrange("g e p -> g p e"))
-            nc.tensor.transpose(backs[k][:, u, :], turned, ident[:])
-
-        def words_of(k):
-            return grouped[k].bitcast(F32).rearrange("p (g u) -> p g u", u=2)
-
-        def slots_of(k):
-            return grouped[k].rearrange("p (g t) -> p g t", t=PACK)
-
-        def reduce_corners(prod, t, k, g0):
-            n = P // 2 if prod.shape[1] < PIECE else P
-            with nc.allow_low_precision(reason="the float32 sum of four products is rounded to bfloat16 once"):
+        def reduce_to_slot(src, points, t, k, g0):
+            with nc.allow_low_precision(reason="the float32 sum is rounded to bfloat16 once"):
                 nc.vector.tensor_reduce(
-                    slots_of(k)[:, g0 : g0 + n, t], prod.rearrange("p (g j) -> p g j", g=n), mybir.AxisListType.X, ADD
+                    slots_of(k)[:, g0 : g0 + points, t], src.rearrange("p (g j) -> p g j", g=points), mybir.AxisListType.X, ADD
                 )
 
-        def pick(t, corners, picked):
-            nc.scalar.activation(picked, window(t, 3 * PIECE, PIECE), COPY)
-            pairs = picked.bitcast(F32).rearrange("p (g u) -> p u g", u=2)
+        def stage(t):
+            words = 5 * HALF + 3 * HALF // 2 + (M * PACK // 2 if t == PACK - 1 else 0)
+            room = held.tile([P, words], F32, name=f"room{t}", tag=f"stage{t}", align_bytes=64)
+            cuts = [0, PIECE, 2 * PIECE, 5 * HALF, 5 * HALF + PIECE // 2, 5 * HALF + 3 * HALF // 2, words]
+            return [room[:, a:b] for a, b in zip(cuts, cuts[1:]) if b > a]
+
+        def turn_chunk0(t, prod):
+            gather(prod, t, 0)
+            add_turned(sums[t // 2][:, t % 2, :], [prod.rearrange("p (g j) -> p j g", j=K)[:, j, :] for j in range(K)])
+
+        def pick_chunk3(t, picked):
+            nc.scalar.activation(picked.bitcast(BF16), window(t, 3 * PIECE, PIECE), COPY)
+            corners = psum.tile([P, 2, P], F32, name=f"corners{t}", tag="corners")
+            pairs = picked.rearrange("p (g u) -> p u g", u=2)
             for u in range(2):
                 nc.tensor.transpose(corners[:, u, :], pairs[:, u, :], ident[:])
-            return corners.rearrange("g u p -> g (u p)").bitcast(BF16).rearrange("g (u p e) -> g u e p", u=2, e=2)
+            return corners[:].rearrange("g u p -> g (u p)").bitcast(BF16).rearrange("g (u p e) -> g u e p", u=2, e=2)
 
-        def weigh(t, corners, weighed):
+        def weigh_chunk3(t, corners):
+            lead = held.tile([P, P], F32, name=f"lead{t}", tag=f"stage{t + 1}", align_bytes=64)
+            rest = held.tile([P, K - 1, P], F32, name=f"rest{t}", tag="rest")
+            weighed = [lead[:]] + [rest[:, j, :] for j in range(K - 1)]
             for j in range(K):
                 nc.scalar.activation(weighed[j], corners[:, j // 2, j % 2, :], COPY, scale=part_last[:, j : j + 1])
             add_turned(direct[:, t, :], weighed)
 
+        def pick_half(t, picked):
+            nc.scalar.activation(picked.bitcast(BF16), window(t, SPREAD - HALF, HALF), COPY)
+            corners = psum.tile([P, P], F32, name=f"half_corners{t}", tag="half_corners")
+            nc.tensor.transpose(corners[:], picked, ident[:])
+            return corners[:].bitcast(BF16).rearrange("g (p e) -> g e p", e=2)
+
+        def weigh_half(t, corners):
+            weighed = held.tile([P, 2, P], F32, name=f"weighed_half{t}", tag="weighed_half")
+            for e in range(2):
+                nc.scalar.activation(weighed[:, e, :], corners[:, e, :], COPY, scale=part_half[:, e : e + 1])
+            half_sums = psum.tile([P, P], F32, name=f"half_sums{t}", tag="half_sums")
+            add_turned(half_sums[:], [weighed[:, e, :] for e in range(2)])
+            return half_sums[:]
+
+        def round_pair(u):
+            turned = held.tile([P, P], F32, name=f"turned{u}", tag="turned")
+            nc.scalar.copy(turned[:].bitcast(BF16).rearrange("g (p e) -> g p e", e=2), sums[u][:].rearrange("g e p -> g p e"))
+            nc.tensor.transpose(backs[:, u, :], turned[:], ident[:])
+
         def leave_direct(u):
             nc.scalar.copy(slots_of(3)[:, :, 2 * u : 2 * u + 2], direct[:, 2 * u : 2 * u + 2, :].rearrange("p t g -> p g t"))
 
-        def stage(t):
-            room = held.tile([P, 4 * PIECE], F32, name=f"room{t}", tag=f"stage{t}", align_bytes=64)
-            prods = [room[:, i * PIECE : (i + 1) * PIECE] for i in range(3)]
-            picked = room[:, 3 * PIECE : 3 * PIECE + PIECE // 2].bitcast(BF16)
-            return prods, picked
-
-        def weighed_tile(t):
-            most = held.tile([P, K - 1, P], F32, name=f"weighed{t}", tag=f"stage{t + 1}", align_bytes=64)
-            last = placed.tile([P, P], F32, name=f"weighed_last{t}", offset=(16 * PIECE, 8 * PIECE, 0)[t], align_bytes=64)
-            return [most[:, j, :] for j in range(K - 1)] + [last[:]]
-
-        for t in range(2):
-            prods, picked = stage(t)
-            corners = pick(t, first[0][:, 2:4, :], picked)
-            gather_and_turn(t, 1, prods[0])
-            gather(prods[1], t, 2 * PIECE)
+        for t in range(PACK - 1):
+            prod0, prod1, prod2, picked3, picked2 = stage(t)
+            half_corners = pick_half(t, picked2)
+            turn_chunk0(t, prod0)
+            corners = pick_chunk3(t, picked3)
+            gather(prod1, t, PIECE)
+            half_sums = weigh_half(t, half_corners)
+            gather(prod2, t, 2 * PIECE)
+            weigh_chunk3(t, corners)
+            reduce_to_slot(prod1, P, t, 1, 0)
+            reduce_to_slot(prod2, P // 2, t, 2, 0)
+            reduce_to_slot(half_sums, P // 2, t, 2, P // 2)
             if t == 1:
-                turned = held.tile([P, P], F32, name="turned1")
-                round_pair(1, 0, turned[:])
-            weigh(t, corners, weighed_tile(t))
-            gather_and_turn(t, 0, prods[2])
-            reduce_corners(prods[1], t, 2, 0)
-        nc.scalar.copy(words_of(1)[:, :, 0], backs[1][:, 0, :])
-        leave_direct(0)
+                round_pair(0)
+                leave_direct(0)
 
-        prods, picked = stage(2)
-        third_corners = psum.tile([P, 2, P], F32, name="third_corners", tag="bank5")
-        corners = pick(2, third_corners[:], picked)
-        plain = placed.tile([P, PIECE], F32, name="plain", offset=8 * PIECE, align_bytes=64)
-        nc.scalar.activation(plain[:], window(2, PIECE, PIECE), COPY)
-        gather(prods[1], 2, 2 * PIECE)
-        gather_and_turn(2, 0, prods[2])
-        reduce_corners(prods[1], 2, 2, 0)
-        for h in range(2):
-            cols = slice(h * half, (h + 1) * half)
-            nc.vector.tensor_tensor(prods[0][:, cols], plain[:, cols], part_rep[:, PIECE + h * half : PIECE + (h + 1) * half], MULT)
-        for h in range(2):
-            reduce_corners(prods[0][:, h * half : (h + 1) * half], 2, 1, h * P // 2)
-        weigh(2, corners, weighed_tile(2))
-        turned = placed.tile([P, P], F32, name="turned0", offset=8 * PIECE, align_bytes=64)
-        round_pair(0, 0, turned[:])
-
-        def quantize(flat, name, codes=None):
+        def quantize(flat, name):
             n = flat.shape[1] // PACK
-            if codes is None:
-                codes = held.tile([P, n], U32, name=f"codes{name}", align_bytes=64)[:]
+            codes = held.tile([P, n], U32, name=f"codes{name}", align_bytes=64)
             scales = held.tile([P, n], U8, name=f"scales{name}", align_bytes=64)
-            nc.vector.quantize_mx(out=codes.bitcast(FP8X4), scales=scales[:], in_=flat)
+            nc.vector.quantize_mx(out=codes[:].bitcast(FP8X4), scales=scales[:], in_=flat)
             return codes, scales
 
-        def finish(name, bank, g0, copy, codes, scales, tag=None):
-            n = codes.shape[1]
-            acc = psum.tile([P, 2, n], F32, name=f"acc{name}", tag=bank)
+        def multiply(acc, m, packed):
+            nc.tensor.matmul_mx(
+                out=acc,
+                lhsT=w_packed[m][0][:].bitcast(FP8X4),
+                lhsT_scale=w_packed[m][1][:],
+                rhs=packed[0][:].bitcast(FP8X4),
+                rhs_scale=packed[1][:],
+                start=True,
+                stop=True,
+            )
+
+        def store(k, result):
+            nc.sync.dma_start(out[:, k * P : (k + 1) * P].rearrange("(m p) g -> p m g", m=2), result[:])
+
+        def finish(k, bank, copy, packed):
+            acc = psum.tile([P, 2, P], F32, name=f"acc{k}", tag=bank)
             for m in range(2):
-                cols = slice(m * P, (m + 1) * P)
-                nc.tensor.matmul_mx(
-                    out=acc[:, m, :],
-                    lhsT=w_codes[:, cols].bitcast(FP8X4),
-                    lhsT_scale=w_scales[:, cols],
-                    rhs=codes.bitcast(FP8X4),
-                    rhs_scale=scales[:],
-                    start=True,
-                    stop=True,
-                )
-            if name == "1":
-                result = placed.tile([P, 2, n], F32, name="result1", offset=W_AT + 3 * PIECE, align_bytes=64)
-            else:
-                result = held.tile([P, 2, n], F32, name=f"result{name}", tag=tag or f"result{name}", align_bytes=64)
+                multiply(acc[:, m, :], m, packed)
+            result = held.tile([P, 2, P], F32, name=f"result{k}", align_bytes=ROW_ALIGN)
             copy(result[:], acc[:])
-            nc.sync.dma_start(out[:, g0 : g0 + n].rearrange("(m p) g -> p m g", m=2), result[:])
+            store(k, result)
 
-        last_corners = psum.tile([P, 2, P], F32, name="last_corners", tag="bank6")
-        prods, picked = stage(3)
-        corners = pick(3, last_corners[:], picked)
-        w_grouped = placed.tile([P, M * PACK], BF16, name="w_grouped", offset=0, align_bytes=64)[:]
-        nc.scalar.copy(
-            w_grouped.rearrange("p (c i t) -> p c t i", i=4, t=PACK), w_raw[:].rearrange("p t (c i) -> p c t i", i=4)
-        )
-        gather_and_turn(3, 0, prods[0])
-        after_w = placed.tile([P, K, P], F32, name="after_w", offset=W_AT, align_bytes=64)
-        last_turned = placed.tile([P, P], F32, name="last_turned", offset=W_AT + 4 * PIECE, align_bytes=64)
-        picked_half = placed.tile([P, half], BF16, name="picked_half", offset=W_AT + 5 * PIECE, align_bytes=64)
-        weighed_half = placed.tile([P, 2, P], F32, name="weighed_half", offset=W_AT + 6 * PIECE, align_bytes=64)
-        nc.scalar.activation(picked_half[:], window(3, FUSED - half, half), COPY)
-        half_corners = psum.tile([P, P], F32, name="half_corners", tag="bank5")
-        nc.tensor.transpose(half_corners[:], picked_half[:].bitcast(F32), ident[:])
-        weigh(3, corners, [after_w[:, j, :] for j in range(K)])
-        round_pair(0, 1, last_turned[:])
-        half_sums = psum.tile([P, P], F32, name="half_sums", tag="bank2")
-        for e in range(2):
-            pairs = half_corners[:].bitcast(BF16).rearrange("g (p e) -> g e p", e=2)
-            nc.scalar.activation(weighed_half[:, e, :], pairs[:, e, :], COPY, scale=part_half[:, e : e + 1])
-        add_turned(half_sums[:], [weighed_half[:, e, :] for e in range(2)])
+        t = PACK - 1
+        prod0, prod1, prod2, picked3, picked2, w_room = stage(t)
+        w_grouped = [w_room[:, m * M : (m + 1) * M].bitcast(BF16) for m in range(2)]
+
+        def round_w(m, copy):
+            copy(
+                w_grouped[m].rearrange("p (c i t) -> p c t i", i=4, t=PACK),
+                w_raw[:, :, m * P : (m + 1) * P].rearrange("p t (c i) -> p c t i", i=4),
+            )
+
+        corners = pick_chunk3(t, picked3)
+        turn_chunk0(t, prod0)
+        half_corners = pick_half(t, picked2)
+        round_w(1, nc.vector.tensor_copy)
+        round_w(0, nc.scalar.copy)
+        for h in range(2):
+            gather(prod1[:, h * HALF : (h + 1) * HALF], t, PIECE + h * HALF)
+        w_second = quantize(w_grouped[1], "w1")
+        weigh_chunk3(t, corners)
+        round_pair(1)
+        half_sums = weigh_half(t, half_corners)
         leave_direct(1)
-        nc.scalar.copy(words_of(0), backs[0].rearrange("p u g -> p g u"))
-
-        prod = prods[1]
+        nc.scalar.copy(grouped[0].bitcast(F32).rearrange("p (g u) -> p g u", u=2), backs[:].rearrange("p u g -> p g u"))
         for h in range(2):
-            gather(prod[:, h * half : (h + 1) * half], 3, PIECE + h * half)
-        for h in range(2):
-            reduce_corners(prod[:, h * half : (h + 1) * half], 3, 1, h * P // 2)
-        nc.vector.quantize_mx(
-            out=w_codes[:].bitcast(FP8X4), scales=w_scales[:], in_=w_grouped
-        )
-        third = placed.tile([P, half], F32, name="third", offset=0, align_bytes=64)
-        gather(third[:], 3, 2 * PIECE)
-        after_wq = placed.tile([P, P], U32, name="after_wq", offset=4 * half, align_bytes=64)
-        finish("1", "bank6", P, nc.scalar.copy, *quantize(grouped[1], "1", after_wq[:]))
-        reduce_corners(third[:], 3, 2, 0)
-        packed20 = quantize(grouped[2][:, :half], "20")
-        finish("3", "bank7", 3 * P, nc.scalar.copy, *quantize(grouped[3], "3"))
-        reduce_corners(half_sums[:], 3, 2, P // 2)
+            reduce_to_slot(prod1[:, h * HALF : (h + 1) * HALF], P // 2, t, 1, h * P // 2)
+        w_packed = [quantize(w_grouped[0], "w0"), w_second]
+        gather(prod2, t, 2 * PIECE)
+        finish(1, "spare", nc.scalar.copy, quantize(grouped[1], "1"))
+        reduce_to_slot(prod2, P // 2, t, 2, 0)
+        finish(3, "sums01", nc.scalar.copy, quantize(grouped[3], "3"))
+        reduce_to_slot(half_sums, P // 2, t, 2, P // 2)
         packed0 = quantize(grouped[0], "0")
-        packed21 = quantize(grouped[2][:, half:], "21")
-        finish("20", "bank5", 2 * P, nc.vector.tensor_copy, *packed20, tag="grouped0")
-        finish("0", "bank1", 0, nc.vector.tensor_copy, *packed0)
-        finish("21", "bank4", 2 * P + P // 2, nc.scalar.copy, *packed21)
+        packed2 = quantize(grouped[2], "2")
+        finish(0, "corners", nc.vector.tensor_copy, packed0)
+        result2 = held.tile([P, 2, P], F32, name="result2", align_bytes=ROW_ALIGN)
+        for m, (bank, copy) in enumerate((("half_corners", nc.scalar.copy), ("sums23", nc.vector.tensor_copy))):
+            acc = psum.tile([P, P], F32, name=f"acc2{m}", tag=bank)
+            multiply(acc[:], m, packed2)
+            copy(result2[:, m, :], acc[:])
+        store(2, result2)

@@ -63,14 +63,17 @@ def tile_attend_grid_kernel(tc, xT, w, part, offs, out):
             copy(part_view[:, :, 4 * b : 4 * b + 4], bank[:].rearrange("p i q -> p q i"))
 
         part_half = held.tile([P, 2], F32, name="part_half")
-        bank = psum.tile([P, 2, P], F32, name="half_bank", tag="direct")
+        bank = psum.tile([P, 2, P], F32, name="half_bank", tag="direct01")
         for e in range(2):
             nc.tensor.transpose(bank[:, e, :], part_rep[:, SPREAD - HALF + e : SPREAD : 2], ident[:])
         nc.vector.tensor_copy(part_half[:], bank[:, :, 0])
 
         sums = [psum.tile([P, 2, P], F32, name=tag, tag=tag) for tag in ("sums01", "sums23")]
         backs = psum.tile([P, 2, P], F32, name="backs", tag="backs")
-        direct = psum.tile([P, PACK, P], F32, name="direct", tag="direct")
+        shared = psum.tile([P, 3, P], F32, name="direct01", tag="direct01")
+        direct = [shared[:, :2, :], psum.tile([P, 2, P], F32, name="direct23", tag="direct23")[:]]
+        half_turned = shared[:, 2, :]
+        half_sums = []
         grouped = [held.tile([P, P * PACK], BF16, name=f"grouped{k}", align_bytes=64)[:] for k in range(G // P)]
 
         def slots_of(k):
@@ -117,21 +120,29 @@ def tile_attend_grid_kernel(tc, xT, w, part, offs, out):
             weighed = [lead[:]] + [rest[:, j, :] for j in range(K - 1)]
             for j in range(K):
                 nc.scalar.activation(weighed[j], corners[:, j // 2, j % 2, :], COPY, scale=part_last[:, j : j + 1])
-            add_turned(direct[:, t, :], weighed)
+            add_turned(direct[t // 2][:, t % 2, :], weighed)
 
         def pick_half(t, picked):
             nc.scalar.activation(picked.bitcast(BF16), window(t, SPREAD - HALF, HALF), COPY)
-            corners = psum.tile([P, P], F32, name=f"half_corners{t}", tag="half_corners")
-            nc.tensor.transpose(corners[:], picked, ident[:])
-            return corners[:].bitcast(BF16).rearrange("g (p e) -> g e p", e=2)
+            nc.tensor.transpose(half_turned, picked, ident[:])
+            return half_turned.bitcast(BF16).rearrange("g (p e) -> g e p", e=2)
 
         def weigh_half(t, corners):
             weighed = held.tile([P, 2, P], F32, name=f"weighed_half{t}", tag="weighed_half")
             for e in range(2):
                 nc.scalar.activation(weighed[:, e, :], corners[:, e, :], COPY, scale=part_half[:, e : e + 1])
-            half_sums = psum.tile([P, P], F32, name=f"half_sums{t}", tag="half_sums")
-            add_turned(half_sums[:], [weighed[:, e, :] for e in range(2)])
-            return half_sums[:]
+            if t % 2 == 0:
+                half_sums.append(psum.tile([P, 2, P], F32, name=f"half_sums{t // 2}", tag="half_sums"))
+            add_turned(half_sums[t // 2][:, t % 2, :], [weighed[:, e, :] for e in range(2)])
+
+        def reduce_half(u):
+            with nc.allow_low_precision(reason="the float32 sum is rounded to bfloat16 once"):
+                nc.vector.tensor_reduce(
+                    slots_of(2)[:, P // 2 :, 2 * u : 2 * u + 2],
+                    half_sums[u][:].rearrange("p t (g v) -> p g t v", v=2),
+                    mybir.AxisListType.X,
+                    ADD,
+                )
 
         def round_pair(u):
             turned = held.tile([P, P], F32, name=f"turned{u}", tag="turned")
@@ -139,7 +150,7 @@ def tile_attend_grid_kernel(tc, xT, w, part, offs, out):
             nc.tensor.transpose(backs[:, u, :], turned[:], ident[:])
 
         def leave_direct(u):
-            nc.scalar.copy(slots_of(3)[:, :, 2 * u : 2 * u + 2], direct[:, 2 * u : 2 * u + 2, :].rearrange("p t g -> p g t"))
+            nc.scalar.copy(slots_of(3)[:, :, 2 * u : 2 * u + 2], direct[u].rearrange("p t g -> p g t"))
 
         for t in range(PACK - 1):
             prod0, prod1, prod2, picked3, picked2 = stage(t)
@@ -147,15 +158,15 @@ def tile_attend_grid_kernel(tc, xT, w, part, offs, out):
             turn_chunk0(t, prod0)
             corners = pick_chunk3(t, picked3)
             gather(prod1, t, PIECE)
-            half_sums = weigh_half(t, half_corners)
+            weigh_half(t, half_corners)
             gather(prod2, t, 2 * PIECE)
             weigh_chunk3(t, corners)
             reduce_to_slot(prod1, P, t, 1, 0)
             reduce_to_slot(prod2, P // 2, t, 2, 0)
-            reduce_to_slot(half_sums, P // 2, t, 2, P // 2)
             if t == 1:
+                reduce_half(0)
                 round_pair(0)
-                leave_direct(0)
+        leave_direct(0)
 
         def quantize(flat, name):
             n = flat.shape[1] // PACK
@@ -186,6 +197,14 @@ def tile_attend_grid_kernel(tc, xT, w, part, offs, out):
             copy(result[:], acc[:])
             store(k, result)
 
+        def finish_shared(k, banks, packed):
+            result = held.tile([P, 2, P], F32, name=f"result{k}", align_bytes=ROW_ALIGN)
+            for m, copy in enumerate((nc.scalar.copy, nc.vector.tensor_copy)):
+                acc = psum.tile([P, P], F32, name=f"acc{k}{m}", tag=banks[m])
+                multiply(acc[:], m, packed)
+                copy(result[:, m, :], acc[:])
+            store(k, result)
+
         t = PACK - 1
         prod0, prod1, prod2, picked3, picked2, w_room = stage(t)
         w_grouped = [w_room[:, m * M : (m + 1) * M].bitcast(BF16) for m in range(2)]
@@ -206,23 +225,18 @@ def tile_attend_grid_kernel(tc, xT, w, part, offs, out):
         w_second = quantize(w_grouped[1], "w1")
         weigh_chunk3(t, corners)
         round_pair(1)
-        half_sums = weigh_half(t, half_corners)
+        weigh_half(t, half_corners)
         leave_direct(1)
         nc.scalar.copy(grouped[0].bitcast(F32).rearrange("p (g u) -> p g u", u=2), backs[:].rearrange("p u g -> p g u"))
         for h in range(2):
             reduce_to_slot(prod1[:, h * HALF : (h + 1) * HALF], P // 2, t, 1, h * P // 2)
         w_packed = [quantize(w_grouped[0], "w0"), w_second]
         gather(prod2, t, 2 * PIECE)
-        finish(1, "spare", nc.scalar.copy, quantize(grouped[1], "1"))
+        finish(1, "sums01", nc.scalar.copy, quantize(grouped[1], "1"))
         reduce_to_slot(prod2, P // 2, t, 2, 0)
-        finish(3, "sums01", nc.scalar.copy, quantize(grouped[3], "3"))
-        reduce_to_slot(half_sums, P // 2, t, 2, P // 2)
+        finish(3, "direct01", nc.scalar.copy, quantize(grouped[3], "3"))
+        reduce_half(1)
         packed0 = quantize(grouped[0], "0")
         packed2 = quantize(grouped[2], "2")
-        finish(0, "corners", nc.vector.tensor_copy, packed0)
-        result2 = held.tile([P, 2, P], F32, name="result2", align_bytes=ROW_ALIGN)
-        for m, (bank, copy) in enumerate((("half_corners", nc.scalar.copy), ("sums23", nc.vector.tensor_copy))):
-            acc = psum.tile([P, P], F32, name=f"acc2{m}", tag=bank)
-            multiply(acc[:], m, packed2)
-            copy(result2[:, m, :], acc[:])
-        store(2, result2)
+        finish_shared(0, ("corners", "spare"), packed0)
+        finish_shared(2, ("sums23", "backs"), packed2)

@@ -154,13 +154,20 @@ def tile_attend_grid_kernel(tc, xT, w, part, offs, out):
 
         for t in range(PACK - 1):
             prod0, prod1, prod2, picked3, picked2 = stage(t)
-            half_corners = pick_half(t, picked2)
-            turn_chunk0(t, prod0)
-            corners = pick_chunk3(t, picked3)
+            if t < 2:
+                half_corners = pick_half(t, picked2)
+                turn_chunk0(t, prod0)
+                corners = pick_chunk3(t, picked3)
+                weigh_half(t, half_corners)
+                weigh_chunk3(t, corners)
+            else:
+                corners = pick_chunk3(t, picked3)
+                turn_chunk0(t, prod0)
+                half_corners = pick_half(t, picked2)
+                weigh_chunk3(t, corners)
+                weigh_half(t, half_corners)
             gather(prod1, t, PIECE)
-            weigh_half(t, half_corners)
             gather(prod2, t, 2 * PIECE)
-            weigh_chunk3(t, corners)
             reduce_to_slot(prod1, P, t, 1, 0)
             reduce_to_slot(prod2, P // 2, t, 2, 0)
             if t == 1:

@@ -26,6 +26,7 @@ PIECE = P * K
 HALF = PIECE // 2
 SPREAD = 3 * PIECE
 ROW_ALIGN = 256
+W_SPLIT = 3 * M // 4
 
 
 def tile_attend_grid_kernel(tc, xT, w, part, offs, out):
@@ -97,10 +98,11 @@ def tile_attend_grid_kernel(tc, xT, w, part, offs, out):
                 )
 
         def stage(t):
-            words = 5 * HALF + 3 * HALF // 2 + (M * PACK // 2 if t == PACK - 1 else 0)
+            cuts = [0, PIECE, 2 * PIECE, 5 * HALF, 5 * HALF + P, 5 * HALF + 3 * P]
+            w_from = cuts[-1]
+            words = w_from + M * PACK // 2 if t == PACK - 1 else cuts[-1]
             room = held.tile([P, words], F32, name=f"room{t}", tag=f"stage{t}", align_bytes=64)
-            cuts = [0, PIECE, 2 * PIECE, 5 * HALF, 5 * HALF + PIECE // 2, 5 * HALF + 3 * HALF // 2, words]
-            return [room[:, a:b] for a, b in zip(cuts, cuts[1:]) if b > a]
+            return [room[:, a:b] for a, b in zip(cuts, cuts[1:])] + [room[:, w_from:]]
 
         def turn_chunk0(t, prod):
             gather(prod, t, 0)
@@ -153,7 +155,7 @@ def tile_attend_grid_kernel(tc, xT, w, part, offs, out):
             nc.scalar.copy(slots_of(3)[:, :, 2 * u : 2 * u + 2], direct[u].rearrange("p t g -> p g t"))
 
         for t in range(PACK - 1):
-            prod0, prod1, prod2, picked3, picked2 = stage(t)
+            prod0, prod1, prod2, picked2, picked3 = stage(t)[:5]
             if t < 2:
                 half_corners = pick_half(t, picked2)
                 turn_chunk0(t, prod0)
@@ -185,8 +187,8 @@ def tile_attend_grid_kernel(tc, xT, w, part, offs, out):
         def multiply(acc, m, packed):
             nc.tensor.matmul_mx(
                 out=acc,
-                lhsT=w_packed[m][0][:].bitcast(FP8X4),
-                lhsT_scale=w_packed[m][1][:],
+                lhsT=w_packed[0][:, m * P : (m + 1) * P].bitcast(FP8X4),
+                lhsT_scale=w_packed[1][:, m * P : (m + 1) * P],
                 rhs=packed[0][:].bitcast(FP8X4),
                 rhs_scale=packed[1][:],
                 start=True,
@@ -213,23 +215,22 @@ def tile_attend_grid_kernel(tc, xT, w, part, offs, out):
             store(k, result)
 
         t = PACK - 1
-        prod0, prod1, prod2, picked3, picked2, w_room = stage(t)
-        w_grouped = [w_room[:, m * M : (m + 1) * M].bitcast(BF16) for m in range(2)]
+        prod0, prod1, prod2, picked2, picked3, w_room = stage(t)
+        w_grouped = w_room.bitcast(BF16)
 
-        def round_w(m, copy):
+        def round_w(m0, m1, copy):
             copy(
-                w_grouped[m].rearrange("p (c i t) -> p c t i", i=4, t=PACK),
-                w_raw[:, :, m * P : (m + 1) * P].rearrange("p t (c i) -> p c t i", i=4),
+                w_grouped[:, m0 * PACK : m1 * PACK].rearrange("p (c i t) -> p c t i", i=4, t=PACK),
+                w_raw[:, :, m0:m1].rearrange("p t (c i) -> p c t i", i=4),
             )
 
         corners = pick_chunk3(t, picked3)
         turn_chunk0(t, prod0)
         half_corners = pick_half(t, picked2)
-        round_w(1, nc.vector.tensor_copy)
-        round_w(0, nc.scalar.copy)
+        round_w(0, W_SPLIT, nc.vector.tensor_copy)
+        round_w(W_SPLIT, M, nc.scalar.copy)
         for h in range(2):
             gather(prod1[:, h * HALF : (h + 1) * HALF], t, PIECE + h * HALF)
-        w_second = quantize(w_grouped[1], "w1")
         weigh_chunk3(t, corners)
         round_pair(1)
         weigh_half(t, half_corners)
@@ -237,13 +238,14 @@ def tile_attend_grid_kernel(tc, xT, w, part, offs, out):
         nc.scalar.copy(grouped[0].bitcast(F32).rearrange("p (g u) -> p g u", u=2), backs[:].rearrange("p u g -> p g u"))
         for h in range(2):
             reduce_to_slot(prod1[:, h * HALF : (h + 1) * HALF], P // 2, t, 1, h * P // 2)
-        w_packed = [quantize(w_grouped[0], "w0"), w_second]
         gather(prod2, t, 2 * PIECE)
+        w_packed = quantize(w_grouped, "w")
         finish(1, "sums01", nc.scalar.copy, quantize(grouped[1], "1"))
         reduce_to_slot(prod2, P // 2, t, 2, 0)
-        finish(3, "direct01", nc.scalar.copy, quantize(grouped[3], "3"))
+        packed3 = quantize(grouped[3], "3")
         reduce_half(1)
         packed0 = quantize(grouped[0], "0")
         packed2 = quantize(grouped[2], "2")
+        finish_shared(3, ("direct01", "direct23"), packed3)
         finish_shared(0, ("corners", "spare"), packed0)
         finish_shared(2, ("sums23", "backs"), packed2)

@@ -71,9 +71,10 @@ def tile_attend_grid_kernel(tc, xT, w, part, offs, out):
 
         sums = [psum.tile([P, 2, P], F32, name=tag, tag=tag) for tag in ("sums01", "sums23")]
         backs = psum.tile([P, 2, P], F32, name="backs", tag="backs")
-        shared = psum.tile([P, 3, P], F32, name="direct01", tag="direct01")
-        direct = [shared[:, :2, :], psum.tile([P, 2, P], F32, name="direct23", tag="direct23")[:]]
-        half_turned = shared[:, 2, :]
+        shared = psum.tile([P, 2, P], F32, name="direct0", tag="direct01")
+        later = psum.tile([P, PACK - 1, P], F32, name="direct123", tag="direct23")
+        direct = [shared[:, 0, :]] + [later[:, t, :] for t in range(PACK - 1)]
+        half_turned = shared[:, 1, :]
         half_sums = []
         grouped = [held.tile([P, P * PACK], BF16, name=f"grouped{k}", align_bytes=64)[:] for k in range(G // P)]
 
@@ -122,7 +123,7 @@ def tile_attend_grid_kernel(tc, xT, w, part, offs, out):
             weighed = [lead[:]] + [rest[:, j, :] for j in range(K - 1)]
             for j in range(K):
                 nc.scalar.activation(weighed[j], corners[:, j // 2, j % 2, :], COPY, scale=part_last[:, j : j + 1])
-            add_turned(direct[t // 2][:, t % 2, :], weighed)
+            add_turned(direct[t], weighed)
 
         def pick_half(t, picked):
             nc.scalar.activation(picked.bitcast(BF16), window(t, SPREAD - HALF, HALF), COPY)
@@ -151,8 +152,6 @@ def tile_attend_grid_kernel(tc, xT, w, part, offs, out):
             nc.scalar.copy(turned[:].bitcast(BF16).rearrange("g (p e) -> g p e", e=2), sums[u][:].rearrange("g e p -> g p e"))
             nc.tensor.transpose(backs[:, u, :], turned[:], ident[:])
 
-        def leave_direct(u):
-            nc.scalar.copy(slots_of(3)[:, :, 2 * u : 2 * u + 2], direct[u].rearrange("p t g -> p g t"))
 
         for t in range(PACK - 1):
             prod0, prod1, prod2, picked2, picked3 = stage(t)[:5]
@@ -174,8 +173,8 @@ def tile_attend_grid_kernel(tc, xT, w, part, offs, out):
             reduce_to_slot(prod2, P // 2, t, 2, 0)
             if t == 1:
                 reduce_half(0)
+                nc.scalar.copy(slots_of(3)[:, :, 0], direct[0])
                 round_pair(0)
-        leave_direct(0)
 
         def quantize(flat, name):
             n = flat.shape[1] // PACK
@@ -234,7 +233,7 @@ def tile_attend_grid_kernel(tc, xT, w, part, offs, out):
         weigh_chunk3(t, corners)
         round_pair(1)
         weigh_half(t, half_corners)
-        leave_direct(1)
+        nc.scalar.copy(slots_of(3)[:, :, 1:], later[:].rearrange("p t g -> p g t"))
         nc.scalar.copy(grouped[0].bitcast(F32).rearrange("p (g u) -> p g u", u=2), backs[:].rearrange("p u g -> p g u"))
         for h in range(2):
             reduce_to_slot(prod1[:, h * HALF : (h + 1) * HALF], P // 2, t, 1, h * P // 2)

@@ -231,8 +231,8 @@ def tile_attend_grid_kernel(tc, xT, w, part, offs, out):
         for h in range(2):
             gather(prod1[:, h * HALF : (h + 1) * HALF], t, PIECE + h * HALF)
         weigh_chunk3(t, corners)
-        round_pair(1)
         weigh_half(t, half_corners)
+        round_pair(1)
         nc.scalar.copy(slots_of(3)[:, :, 1:], later[:].rearrange("p t g -> p g t"))
         nc.scalar.copy(grouped[0].bitcast(F32).rearrange("p (g u) -> p g u", u=2), backs[:].rearrange("p u g -> p g u"))
         for h in range(2):
@@ -241,10 +241,10 @@ def tile_attend_grid_kernel(tc, xT, w, part, offs, out):
         w_packed = quantize(w_grouped, "w")
         finish(1, "sums01", nc.scalar.copy, quantize(grouped[1], "1"))
         reduce_to_slot(prod2, P // 2, t, 2, 0)
-        packed3 = quantize(grouped[3], "3")
         reduce_half(1)
-        packed0 = quantize(grouped[0], "0")
+        packed3 = quantize(grouped[3], "3")
         packed2 = quantize(grouped[2], "2")
+        packed0 = quantize(grouped[0], "0")
         finish_shared(3, ("direct01", "direct23"), packed3)
-        finish_shared(0, ("corners", "spare"), packed0)
-        finish_shared(2, ("sums23", "backs"), packed2)
+        finish_shared(2, ("corners", "spare"), packed2)
+        finish_shared(0, ("sums23", "half_sums"), packed0)

@@ -26,7 +26,7 @@ PIECE = P * K
 HALF = PIECE // 2
 SPREAD = 3 * PIECE
 ROW_ALIGN = 256
-W_SPLIT = 3 * M // 4
+W_SPLIT = 5 * M // 8
 
 
 def tile_attend_grid_kernel(tc, xT, w, part, offs, out):
@@ -147,10 +147,13 @@ def tile_attend_grid_kernel(tc, xT, w, part, offs, out):
                     ADD,
                 )
 
-        def round_pair(u):
-            turned = held.tile([P, P], F32, name=f"turned{u}", tag="turned")
-            nc.scalar.copy(turned[:].bitcast(BF16).rearrange("g (p e) -> g p e", e=2), sums[u][:].rearrange("g e p -> g p e"))
-            nc.tensor.transpose(backs[:, u, :], turned[:], ident[:])
+        turned = [held.tile([P, P], F32, name=f"turned{u}")[:] for u in range(2)]
+
+        def round_sums(u, e0, e1):
+            pairs = turned[u].bitcast(BF16).rearrange("g (p e) -> g p e", e=2)
+            nc.scalar.copy(pairs[:, :, e0:e1], sums[u][:, e0:e1, :].rearrange("g e p -> g p e"))
+            if e1 == 2:
+                nc.tensor.transpose(backs[:, u, :], turned[u], ident[:])
 
 
         for t in range(PACK - 1):
@@ -174,7 +177,8 @@ def tile_attend_grid_kernel(tc, xT, w, part, offs, out):
             if t == 1:
                 reduce_half(0)
                 nc.scalar.copy(slots_of(3)[:, :, 0], direct[0])
-                round_pair(0)
+                round_sums(0, 0, 2)
+        round_sums(1, 0, 1)
 
         def quantize(flat, name):
             n = flat.shape[1] // PACK
@@ -226,17 +230,15 @@ def tile_attend_grid_kernel(tc, xT, w, part, offs, out):
         corners = pick_chunk3(t, picked3)
         turn_chunk0(t, prod0)
         half_corners = pick_half(t, picked2)
+        gather(prod1, t, PIECE)
         round_w(0, W_SPLIT, nc.vector.tensor_copy)
         round_w(W_SPLIT, M, nc.scalar.copy)
-        for h in range(2):
-            gather(prod1[:, h * HALF : (h + 1) * HALF], t, PIECE + h * HALF)
         weigh_chunk3(t, corners)
         weigh_half(t, half_corners)
-        round_pair(1)
+        round_sums(1, 1, 2)
         nc.scalar.copy(slots_of(3)[:, :, 1:], later[:].rearrange("p t g -> p g t"))
         nc.scalar.copy(grouped[0].bitcast(F32).rearrange("p (g u) -> p g u", u=2), backs[:].rearrange("p u g -> p g u"))
-        for h in range(2):
-            reduce_to_slot(prod1[:, h * HALF : (h + 1) * HALF], P // 2, t, 1, h * P // 2)
+        reduce_to_slot(prod1, P, t, 1, 0)
         gather(prod2, t, 2 * PIECE)
         w_packed = quantize(w_grouped, "w")
         finish(1, "sums01", nc.scalar.copy, quantize(grouped[1], "1"))

@@ -67,7 +67,7 @@ def tile_attend_grid_kernel(tc, xT, w, part, offs, out):
         bank = psum.tile([P, 2, P], F32, name="half_bank", tag="direct01")
         for e in range(2):
             nc.tensor.transpose(bank[:, e, :], part_rep[:, SPREAD - HALF + e : SPREAD : 2], ident[:])
-        nc.vector.tensor_copy(part_half[:], bank[:, :, 0])
+        nc.scalar.copy(part_half[:], bank[:, :, 0])
 
         sums = [psum.tile([P, 2, P], F32, name=tag, tag=tag) for tag in ("sums01", "sums23")]
         backs = psum.tile([P, 2, P], F32, name="backs", tag="backs")
@@ -138,11 +138,11 @@ def tile_attend_grid_kernel(tc, xT, w, part, offs, out):
                 half_sums.append(psum.tile([P, 2, P], F32, name=f"half_sums{t // 2}", tag="half_sums"))
             add_turned(half_sums[t // 2][:, t % 2, :], [weighed[:, e, :] for e in range(2)])
 
-        def reduce_half(u):
+        def reduce_half(t0, t1):
             with nc.allow_low_precision(reason="the float32 sum is rounded to bfloat16 once"):
                 nc.vector.tensor_reduce(
-                    slots_of(2)[:, P // 2 :, 2 * u : 2 * u + 2],
-                    half_sums[u][:].rearrange("p t (g v) -> p g t v", v=2),
+                    slots_of(2)[:, P // 2 :, t0:t1],
+                    half_sums[t0 // 2][:, t0 % 2 : t0 % 2 + t1 - t0, :].rearrange("p t (g v) -> p g t v", v=2),
                     mybir.AxisListType.X,
                     ADD,
                 )
@@ -158,27 +158,21 @@ def tile_attend_grid_kernel(tc, xT, w, part, offs, out):
 
         for t in range(PACK - 1):
             prod0, prod1, prod2, picked2, picked3 = stage(t)[:5]
-            if t < 2:
-                half_corners = pick_half(t, picked2)
-                turn_chunk0(t, prod0)
-                corners = pick_chunk3(t, picked3)
-                weigh_half(t, half_corners)
-                weigh_chunk3(t, corners)
-            else:
-                corners = pick_chunk3(t, picked3)
-                turn_chunk0(t, prod0)
-                half_corners = pick_half(t, picked2)
-                weigh_chunk3(t, corners)
-                weigh_half(t, half_corners)
+            half_corners = pick_half(t, picked2)
+            turn_chunk0(t, prod0)
+            corners = pick_chunk3(t, picked3)
+            weigh_half(t, half_corners)
+            weigh_chunk3(t, corners)
             gather(prod1, t, PIECE)
             gather(prod2, t, 2 * PIECE)
             reduce_to_slot(prod1, P, t, 1, 0)
             reduce_to_slot(prod2, P // 2, t, 2, 0)
             if t == 1:
-                reduce_half(0)
+                reduce_half(0, 2)
                 nc.scalar.copy(slots_of(3)[:, :, 0], direct[0])
                 round_sums(0, 0, 2)
         round_sums(1, 0, 1)
+        reduce_half(2, 3)
 
         def quantize(flat, name):
             n = flat.shape[1] // PACK
@@ -243,7 +237,7 @@ def tile_attend_grid_kernel(tc, xT, w, part, offs, out):
         w_packed = quantize(w_grouped, "w")
         finish(1, "sums01", nc.scalar.copy, quantize(grouped[1], "1"))
         reduce_to_slot(prod2, P // 2, t, 2, 0)
-        reduce_half(1)
+        reduce_half(3, 4)
         packed3 = quantize(grouped[3], "3")
         packed2 = quantize(grouped[2], "2")
         packed0 = quantize(grouped[0], "0")

@@ -1,4 +1,5 @@
 from contextlib import ExitStack
+from itertools import accumulate
 
 import concourse.mybir as mybir
 from concourse.masks import make_identity
@@ -63,11 +64,9 @@ def tile_attend_grid_kernel(tc, xT, w, part, offs, out):
             copy = nc.scalar.copy if b == 0 else nc.vector.tensor_copy
             copy(part_view[:, :, 4 * b : 4 * b + 4], bank[:].rearrange("p i q -> p q i"))
 
-        part_half = held.tile([P, 2], F32, name="part_half")
-        bank = psum.tile([P, 2, P], F32, name="half_bank", tag="direct01")
+        half_bank = psum.tile([P, 2, P], F32, name="half_bank", tag="half_sums")
         for e in range(2):
-            nc.tensor.transpose(bank[:, e, :], part_rep[:, SPREAD - HALF + e : SPREAD : 2], ident[:])
-        nc.scalar.copy(part_half[:], bank[:, :, 0])
+            nc.tensor.transpose(half_bank[:, e, :], part_rep[:, SPREAD - HALF + e : SPREAD : 2], ident[:])
 
         sums = [psum.tile([P, 2, P], F32, name=tag, tag=tag) for tag in ("sums01", "sums23")]
         backs = psum.tile([P, 2, P], F32, name="backs", tag="backs")
@@ -98,12 +97,10 @@ def tile_attend_grid_kernel(tc, xT, w, part, offs, out):
                     slots_of(k)[:, g0 : g0 + points, t], src.rearrange("p (g j) -> p g j", g=points), mybir.AxisListType.X, ADD
                 )
 
-        def stage(t):
-            cuts = [0, PIECE, 2 * PIECE, 5 * HALF, 5 * HALF + P, 5 * HALF + 3 * P]
-            w_from = cuts[-1]
-            words = w_from + M * PACK // 2 if t == PACK - 1 else cuts[-1]
-            room = held.tile([P, words], F32, name=f"room{t}", tag=f"stage{t}", align_bytes=64)
-            return [room[:, a:b] for a, b in zip(cuts, cuts[1:])] + [room[:, w_from:]]
+        def carve(name, widths):
+            ends = list(accumulate(widths, initial=0))
+            room = held.tile([P, ends[-1]], F32, name=name, tag=name, align_bytes=64)
+            return [room[:, a:b] for a, b in zip(ends, ends[1:])]
 
         def turn_chunk0(t, prod):
             gather(prod, t, 0)
@@ -131,7 +128,7 @@ def tile_attend_grid_kernel(tc, xT, w, part, offs, out):
             return half_turned.bitcast(BF16).rearrange("g (p e) -> g e p", e=2)
 
         def weigh_half(t, corners):
-            weighed = held.tile([P, 2, P], F32, name=f"weighed_half{t}", tag="weighed_half")
+            weighed = held.tile([P, 2, P], F32, name=f"weighed_half{t}", tag=f"products{t + 1}", align_bytes=64)
             for e in range(2):
                 nc.scalar.activation(weighed[:, e, :], corners[:, e, :], COPY, scale=part_half[:, e : e + 1])
             if t % 2 == 0:
@@ -157,10 +154,14 @@ def tile_attend_grid_kernel(tc, xT, w, part, offs, out):
 
 
         for t in range(PACK - 1):
-            prod0, prod1, prod2, picked2, picked3 = stage(t)[:5]
+            prod0, prod1, prod2 = carve(f"products{t}", [PIECE, PIECE, HALF])
+            picked2, picked3 = carve(f"stage{t}", [P, 2 * P])
             half_corners = pick_half(t, picked2)
             turn_chunk0(t, prod0)
             corners = pick_chunk3(t, picked3)
+            if t == 0:
+                part_half = picked2[:, :2]
+                nc.scalar.copy(part_half, half_bank[:, :, 0])
             weigh_half(t, half_corners)
             weigh_chunk3(t, corners)
             gather(prod1, t, PIECE)
@@ -212,7 +213,8 @@ def tile_attend_grid_kernel(tc, xT, w, part, offs, out):
             store(k, result)
 
         t = PACK - 1
-        prod0, prod1, prod2, picked2, picked3, w_room = stage(t)
+        prod0, prod1, prod2, w_room = carve(f"products{t}", [PIECE, PIECE, HALF, M * PACK // 2])
+        picked2, picked3 = carve(f"stage{t}", [P, 2 * P])
         w_grouped = w_room.bitcast(BF16)
 
         def round_w(m0, m1, copy):

@@ -20,14 +20,15 @@ D = 512
 M = 256
 G = 512
 K = 4
-E = G * K
 PACK = 4
 FLOPS = 2 * D * M * G
 PIECE = P * K
 HALF = PIECE // 2
 SPREAD = 3 * PIECE
+BANK_TURNS = 4
+MX_ALIGN = 64
 ROW_ALIGN = 256
-W_SPLIT = 5 * M // 8
+W_SPLIT = 9 * M // 16
 
 
 def tile_attend_grid_kernel(tc, xT, w, part, offs, out):
@@ -37,9 +38,9 @@ def tile_attend_grid_kernel(tc, xT, w, part, offs, out):
         held = ctx.enter_context(tc.tile_pool(name="held", bufs=1))
         psum = ctx.enter_context(tc.psum_pool(name="psum", bufs=1))
 
-        offsets = held.tile([P, E // 16], U16, name="offsets")
+        offsets = held.tile([P, G * K // 16], U16, name="offsets")
         nc.sync.dma_start(offsets[:], offs)
-        part_col = held.tile([P, SPREAD // P], F32, name="part_col", tag="stage0", align_bytes=64)
+        part_col = held.tile([P, SPREAD // P], F32, name="part_col", tag="picks0", align_bytes=MX_ALIGN)
         nc.scalar.dma_start(part_col[:], part[0:1, :SPREAD].rearrange("o (q i) -> (o q) i", i=SPREAD // P))
         part_last = held.tile([P, K], F32, name="part_last")
         nc.scalar.dma_start(part_last[:], part[0:1, SPREAD:].rearrange("o (g j) -> (o g) j", j=K))
@@ -54,30 +55,30 @@ def tile_attend_grid_kernel(tc, xT, w, part, offs, out):
         ident = held.tile([P, P], F32, name="ident")
         make_identity(nc, ident[:])
 
-        part_rep = held.tile([P, SPREAD], F32, name="part_rep", align_bytes=64)
+        part_rep = held.tile([P, SPREAD], F32, name="part_rep", align_bytes=MX_ALIGN)
         part_view = part_rep[:].rearrange("p (q i) -> p q i", i=SPREAD // P)
         for b, tag in enumerate(("sums01", "sums23", "backs")):
-            bank = psum.tile([P, 4, P], F32, name=f"part_bank{b}", tag=tag)
-            for i in range(4):
-                col = part_col[:, 4 * b + i : 4 * b + i + 1]
+            bank = psum.tile([P, BANK_TURNS, P], F32, name=f"part_bank{b}", tag=tag)
+            for i in range(BANK_TURNS):
+                col = part_col[:, BANK_TURNS * b + i : BANK_TURNS * b + i + 1]
                 nc.tensor.transpose(bank[:, i, :], col.to_broadcast([P, P]), ident[:])
             copy = nc.scalar.copy if b == 0 else nc.vector.tensor_copy
-            copy(part_view[:, :, 4 * b : 4 * b + 4], bank[:].rearrange("p i q -> p q i"))
+            copy(part_view[:, :, BANK_TURNS * b : BANK_TURNS * (b + 1)], bank[:].rearrange("p i q -> p q i"))
 
-        half_bank = psum.tile([P, 2, P], F32, name="half_bank", tag="half_sums")
+        half_weights = psum.tile([P, 2, P], F32, name="half_weights", tag="half_sums")
         for e in range(2):
-            nc.tensor.transpose(half_bank[:, e, :], part_rep[:, SPREAD - HALF + e : SPREAD : 2], ident[:])
+            nc.tensor.transpose(half_weights[:, e, :], part_rep[:, SPREAD - HALF + e : SPREAD : 2], ident[:])
 
         sums = [psum.tile([P, 2, P], F32, name=tag, tag=tag) for tag in ("sums01", "sums23")]
         backs = psum.tile([P, 2, P], F32, name="backs", tag="backs")
-        shared = psum.tile([P, 2, P], F32, name="direct0", tag="direct01")
-        later = psum.tile([P, PACK - 1, P], F32, name="direct123", tag="direct23")
+        shared = psum.tile([P, 2, P], F32, name="shared", tag="shared")
+        later = psum.tile([P, PACK - 1, P], F32, name="later", tag="later")
         direct = [shared[:, 0, :]] + [later[:, t, :] for t in range(PACK - 1)]
         half_turned = shared[:, 1, :]
         half_sums = []
-        grouped = [held.tile([P, P * PACK], BF16, name=f"grouped{k}", align_bytes=64)[:] for k in range(G // P)]
+        grouped = [held.tile([P, P * PACK], BF16, name=f"grouped{k}", align_bytes=MX_ALIGN)[:] for k in range(G // P)]
 
-        def slots_of(k):
+        def places_of(k):
             return grouped[k].rearrange("p (g t) -> p g t", t=PACK)
 
         def window(t, e0, n):
@@ -91,15 +92,16 @@ def tile_attend_grid_kernel(tc, xT, w, part, offs, out):
             for j, tile in enumerate(tiles):
                 nc.tensor.matmul(acc, tile, ident[:], start=(j == 0), stop=(j == len(tiles) - 1), is_transpose=True)
 
-        def reduce_to_slot(src, points, t, k, g0):
+        def reduce_corners(prod, t, k):
+            points = prod.shape[1] // K
             with nc.allow_low_precision(reason="the float32 sum is rounded to bfloat16 once"):
                 nc.vector.tensor_reduce(
-                    slots_of(k)[:, g0 : g0 + points, t], src.rearrange("p (g j) -> p g j", g=points), mybir.AxisListType.X, ADD
+                    places_of(k)[:, :points, t], prod.rearrange("p (g j) -> p g j", j=K), mybir.AxisListType.X, ADD
                 )
 
         def carve(name, widths):
             ends = list(accumulate(widths, initial=0))
-            room = held.tile([P, ends[-1]], F32, name=name, tag=name, align_bytes=64)
+            room = held.tile([P, ends[-1]], F32, name=name, tag=name, align_bytes=MX_ALIGN)
             return [room[:, a:b] for a, b in zip(ends, ends[1:])]
 
         def turn_chunk0(t, prod):
@@ -115,7 +117,7 @@ def tile_attend_grid_kernel(tc, xT, w, part, offs, out):
             return corners[:].rearrange("g u p -> g (u p)").bitcast(BF16).rearrange("g (u p e) -> g u e p", u=2, e=2)
 
         def weigh_chunk3(t, corners):
-            lead = held.tile([P, P], F32, name=f"lead{t}", tag=f"stage{t + 1}", align_bytes=64)
+            lead = held.tile([P, P], F32, name=f"lead{t}", tag=f"picks{t + 1}", align_bytes=MX_ALIGN)
             rest = held.tile([P, K - 1, P], F32, name=f"rest{t}", tag="rest")
             weighed = [lead[:]] + [rest[:, j, :] for j in range(K - 1)]
             for j in range(K):
@@ -125,12 +127,12 @@ def tile_attend_grid_kernel(tc, xT, w, part, offs, out):
         def pick_half(t, picked):
             nc.scalar.activation(picked.bitcast(BF16), window(t, SPREAD - HALF, HALF), COPY)
             nc.tensor.transpose(half_turned, picked, ident[:])
-            return half_turned.bitcast(BF16).rearrange("g (p e) -> g e p", e=2)
+            return half_turned.bitcast(BF16).rearrange("r (p e) -> r e p", e=2)
 
-        def weigh_half(t, corners):
-            weighed = held.tile([P, 2, P], F32, name=f"weighed_half{t}", tag=f"products{t + 1}", align_bytes=64)
+        def weigh_half(t, entries):
+            weighed = held.tile([P, 2, P], F32, name=f"weighed_half{t}", tag=f"products{t + 1}", align_bytes=MX_ALIGN)
             for e in range(2):
-                nc.scalar.activation(weighed[:, e, :], corners[:, e, :], COPY, scale=part_half[:, e : e + 1])
+                nc.scalar.activation(weighed[:, e, :], entries[:, e, :], COPY, scale=part_half[:, e : e + 1])
             if t % 2 == 0:
                 half_sums.append(psum.tile([P, 2, P], F32, name=f"half_sums{t // 2}", tag="half_sums"))
             add_turned(half_sums[t // 2][:, t % 2, :], [weighed[:, e, :] for e in range(2)])
@@ -138,8 +140,8 @@ def tile_attend_grid_kernel(tc, xT, w, part, offs, out):
         def reduce_half(t0, t1):
             with nc.allow_low_precision(reason="the float32 sum is rounded to bfloat16 once"):
                 nc.vector.tensor_reduce(
-                    slots_of(2)[:, P // 2 :, t0:t1],
-                    half_sums[t0 // 2][:, t0 % 2 : t0 % 2 + t1 - t0, :].rearrange("p t (g v) -> p g t v", v=2),
+                    places_of(2)[:, P // 2 :, t0:t1],
+                    half_sums[t0 // 2][:, t0 % 2 : t0 % 2 + t1 - t0, :].rearrange("p t (g u) -> p g t u", u=2),
                     mybir.AxisListType.X,
                     ADD,
                 )
@@ -152,41 +154,40 @@ def tile_attend_grid_kernel(tc, xT, w, part, offs, out):
             if e1 == 2:
                 nc.tensor.transpose(backs[:, u, :], turned[u], ident[:])
 
-
         for t in range(PACK - 1):
             prod0, prod1, prod2 = carve(f"products{t}", [PIECE, PIECE, HALF])
-            picked2, picked3 = carve(f"stage{t}", [P, 2 * P])
-            half_corners = pick_half(t, picked2)
+            picked2, picked3 = carve(f"picks{t}", [HALF // 2, PIECE // 2])
+            half_entries = pick_half(t, picked2)
             turn_chunk0(t, prod0)
             corners = pick_chunk3(t, picked3)
             if t == 0:
                 part_half = picked2[:, :2]
-                nc.scalar.copy(part_half, half_bank[:, :, 0])
-            weigh_half(t, half_corners)
+                nc.scalar.copy(part_half, half_weights[:, :, 0])
+            weigh_half(t, half_entries)
             weigh_chunk3(t, corners)
             gather(prod1, t, PIECE)
             gather(prod2, t, 2 * PIECE)
-            reduce_to_slot(prod1, P, t, 1, 0)
-            reduce_to_slot(prod2, P // 2, t, 2, 0)
+            reduce_corners(prod1, t, 1)
+            reduce_corners(prod2, t, 2)
             if t == 1:
                 reduce_half(0, 2)
-                nc.scalar.copy(slots_of(3)[:, :, 0], direct[0])
+                nc.scalar.copy(places_of(3)[:, :, 0], direct[0])
                 round_sums(0, 0, 2)
         round_sums(1, 0, 1)
         reduce_half(2, 3)
 
         def quantize(flat, name):
             n = flat.shape[1] // PACK
-            codes = held.tile([P, n], U32, name=f"codes{name}", align_bytes=64)
-            scales = held.tile([P, n], U8, name=f"scales{name}", align_bytes=64)
+            codes = held.tile([P, n], U32, name=f"codes{name}", align_bytes=MX_ALIGN)
+            scales = held.tile([P, n], U8, name=f"scales{name}", align_bytes=MX_ALIGN)
             nc.vector.quantize_mx(out=codes[:].bitcast(FP8X4), scales=scales[:], in_=flat)
             return codes, scales
 
-        def multiply(acc, m, packed):
+        def multiply(acc, h, packed):
             nc.tensor.matmul_mx(
                 out=acc,
-                lhsT=w_packed[0][:, m * P : (m + 1) * P].bitcast(FP8X4),
-                lhsT_scale=w_packed[1][:, m * P : (m + 1) * P],
+                lhsT=w_packed[0][:, h * P : (h + 1) * P].bitcast(FP8X4),
+                lhsT_scale=w_packed[1][:, h * P : (h + 1) * P],
                 rhs=packed[0][:].bitcast(FP8X4),
                 rhs_scale=packed[1][:],
                 start=True,
@@ -194,27 +195,19 @@ def tile_attend_grid_kernel(tc, xT, w, part, offs, out):
             )
 
         def store(k, result):
-            nc.sync.dma_start(out[:, k * P : (k + 1) * P].rearrange("(m p) g -> p m g", m=2), result[:])
-
-        def finish(k, bank, copy, packed):
-            acc = psum.tile([P, 2, P], F32, name=f"acc{k}", tag=bank)
-            for m in range(2):
-                multiply(acc[:, m, :], m, packed)
-            result = held.tile([P, 2, P], F32, name=f"result{k}", align_bytes=ROW_ALIGN)
-            copy(result[:], acc[:])
-            store(k, result)
+            nc.sync.dma_start(out[:, k * P : (k + 1) * P].rearrange("(h p) g -> p h g", h=2), result[:])
 
         def finish_shared(k, banks, packed):
             result = held.tile([P, 2, P], F32, name=f"result{k}", align_bytes=ROW_ALIGN)
-            for m, copy in enumerate((nc.scalar.copy, nc.vector.tensor_copy)):
-                acc = psum.tile([P, P], F32, name=f"acc{k}{m}", tag=banks[m])
-                multiply(acc[:], m, packed)
-                copy(result[:, m, :], acc[:])
+            for h, copy in enumerate((nc.scalar.copy, nc.vector.tensor_copy)):
+                acc = psum.tile([P, P], F32, name=f"acc{k}{h}", tag=banks[h])
+                multiply(acc[:], h, packed)
+                copy(result[:, h, :], acc[:])
             store(k, result)
 
         t = PACK - 1
-        prod0, prod1, prod2, w_room = carve(f"products{t}", [PIECE, PIECE, HALF, M * PACK // 2])
-        picked2, picked3 = carve(f"stage{t}", [P, 2 * P])
+        prod0, prod12, w_room = carve(f"products{t}", [PIECE, PIECE + HALF, M * PACK // 2])
+        picked2, picked3 = carve(f"picks{t}", [HALF // 2, PIECE // 2])
         w_grouped = w_room.bitcast(BF16)
 
         def round_w(m0, m1, copy):
@@ -225,24 +218,29 @@ def tile_attend_grid_kernel(tc, xT, w, part, offs, out):
 
         corners = pick_chunk3(t, picked3)
         turn_chunk0(t, prod0)
-        half_corners = pick_half(t, picked2)
-        gather(prod1, t, PIECE)
+        half_entries = pick_half(t, picked2)
+        gather(prod12, t, PIECE)
         round_w(0, W_SPLIT, nc.vector.tensor_copy)
         round_w(W_SPLIT, M, nc.scalar.copy)
         weigh_chunk3(t, corners)
-        weigh_half(t, half_corners)
+        weigh_half(t, half_entries)
         round_sums(1, 1, 2)
-        nc.scalar.copy(slots_of(3)[:, :, 1:], later[:].rearrange("p t g -> p g t"))
+        nc.scalar.copy(places_of(3)[:, :, 1:], later[:].rearrange("p t g -> p g t"))
         nc.scalar.copy(grouped[0].bitcast(F32).rearrange("p (g u) -> p g u", u=2), backs[:].rearrange("p u g -> p g u"))
-        reduce_to_slot(prod1, P, t, 1, 0)
-        gather(prod2, t, 2 * PIECE)
+        reduce_corners(prod12[:, :PIECE], t, 1)
         w_packed = quantize(w_grouped, "w")
-        finish(1, "sums01", nc.scalar.copy, quantize(grouped[1], "1"))
-        reduce_to_slot(prod2, P // 2, t, 2, 0)
+
+        packed1 = quantize(grouped[1], "1")
+        acc = psum.tile([P, 2, P], F32, name="acc1", tag="sums01")
+        for h in range(2):
+            multiply(acc[:, h, :], h, packed1)
+        result = held.tile([P, 2, P], F32, name="result1", align_bytes=ROW_ALIGN)
+        nc.scalar.copy(result[:], acc[:])
+        store(1, result)
+
+        reduce_corners(prod12[:, PIECE:], t, 2)
         reduce_half(3, 4)
-        packed3 = quantize(grouped[3], "3")
-        packed2 = quantize(grouped[2], "2")
-        packed0 = quantize(grouped[0], "0")
-        finish_shared(3, ("direct01", "direct23"), packed3)
-        finish_shared(2, ("corners", "spare"), packed2)
-        finish_shared(0, ("sums23", "half_sums"), packed0)
+        packed = {k: quantize(grouped[k], str(k)) for k in (3, 2, 0)}
+        finish_shared(3, ("shared", "later"), packed[3])
+        finish_shared(2, ("corners", "spare"), packed[2])
+        finish_shared(0, ("sums23", "half_sums"), packed[0])

from contextlib import ExitStack
from itertools import accumulate

import concourse.mybir as mybir
from concourse.masks import make_identity

F32 = mybir.dt.float32
BF16 = mybir.dt.bfloat16
U32 = mybir.dt.uint32
U16 = mybir.dt.uint16
U8 = mybir.dt.uint8
FP8X4 = mybir.dt.float8_e4m3fn_x4
MULT = mybir.AluOpType.mult
ADD = mybir.AluOpType.add
COPY = mybir.ActivationFunctionType.Copy

P = 128
T = 4096
D = 512
M = 256
G = 512
K = 4
PACK = 4
FLOPS = 2 * D * M * G
PIECE = P * K
HALF = PIECE // 2
SPREAD = 3 * PIECE
BANK_TURNS = 4
MX_ALIGN = 64
ROW_ALIGN = 256
W_SPLIT = 9 * M // 16


def tile_attend_grid_kernel(tc, xT, w, part, offs, out):
    nc = tc.nc
    x_planes = xT.rearrange("(p t) c -> p t c", t=PACK)
    with ExitStack() as ctx:
        held = ctx.enter_context(tc.tile_pool(name="held", bufs=1))
        psum = ctx.enter_context(tc.psum_pool(name="psum", bufs=1))

        offsets = held.tile([P, G * K // 16], U16, name="offsets")
        nc.sync.dma_start(offsets[:], offs)
        part_col = held.tile([P, SPREAD // P], F32, name="part_col", tag="picks0", align_bytes=MX_ALIGN)
        nc.scalar.dma_start(part_col[:], part[0:1, :SPREAD].rearrange("o (q i) -> (o q) i", i=SPREAD // P))
        part_last = held.tile([P, K], F32, name="part_last")
        nc.scalar.dma_start(part_last[:], part[0:1, SPREAD:].rearrange("o (g j) -> (o g) j", j=K))
        planes = []
        for t in range(PACK):
            plane = held.tile([P, T], F32, name=f"plane{t}", align_bytes=ROW_ALIGN)
            nc.sync.dma_start(plane[:], x_planes[:, t, :])
            planes.append(plane)
        w_raw = held.tile([P, PACK, M], F32, name="w_raw", align_bytes=ROW_ALIGN)
        nc.sync.dma_start(w_raw[:], w.rearrange("(p t) m -> p t m", t=PACK))

        ident = held.tile([P, P], F32, name="ident")
        make_identity(nc, ident[:])

        part_rep = held.tile([P, SPREAD], F32, name="part_rep", align_bytes=MX_ALIGN)
        part_view = part_rep[:].rearrange("p (q i) -> p q i", i=SPREAD // P)
        for b, tag in enumerate(("sums01", "sums23", "backs")):
            bank = psum.tile([P, BANK_TURNS, P], F32, name=f"part_bank{b}", tag=tag)
            for i in range(BANK_TURNS):
                col = part_col[:, BANK_TURNS * b + i : BANK_TURNS * b + i + 1]
                nc.tensor.transpose(bank[:, i, :], col.to_broadcast([P, P]), ident[:])
            copy = nc.scalar.copy if b == 0 else nc.vector.tensor_copy
            copy(part_view[:, :, BANK_TURNS * b : BANK_TURNS * (b + 1)], bank[:].rearrange("p i q -> p q i"))

        half_weights = psum.tile([P, 2, P], F32, name="half_weights", tag="half_sums")
        for e in range(2):
            nc.tensor.transpose(half_weights[:, e, :], part_rep[:, SPREAD - HALF + e : SPREAD : 2], ident[:])

        sums = [psum.tile([P, 2, P], F32, name=tag, tag=tag) for tag in ("sums01", "sums23")]
        backs = psum.tile([P, 2, P], F32, name="backs", tag="backs")
        shared = psum.tile([P, 2, P], F32, name="shared", tag="shared")
        later = psum.tile([P, PACK - 1, P], F32, name="later", tag="later")
        direct = [shared[:, 0, :]] + [later[:, t, :] for t in range(PACK - 1)]
        half_turned = shared[:, 1, :]
        half_sums = []
        grouped = [held.tile([P, P * PACK], BF16, name=f"grouped{k}", align_bytes=MX_ALIGN)[:] for k in range(G // P)]

        def places_of(k):
            return grouped[k].rearrange("p (g t) -> p g t", t=PACK)

        def window(t, e0, n):
            return planes[t][:].indirect(offsets[:, e0 // 16 : (e0 + n) // 16])

        def gather(prod, t, e0):
            n = prod.shape[1]
            nc.vector.tensor_tensor(prod, window(t, e0, n), part_rep[:, e0 : e0 + n], MULT)

        def add_turned(acc, tiles):
            for j, tile in enumerate(tiles):
                nc.tensor.matmul(acc, tile, ident[:], start=(j == 0), stop=(j == len(tiles) - 1), is_transpose=True)

        def reduce_corners(prod, t, k):
            points = prod.shape[1] // K
            with nc.allow_low_precision(reason="the float32 sum is rounded to bfloat16 once"):
                nc.vector.tensor_reduce(
                    places_of(k)[:, :points, t], prod.rearrange("p (g j) -> p g j", j=K), mybir.AxisListType.X, ADD
                )

        def carve(name, widths):
            ends = list(accumulate(widths, initial=0))
            room = held.tile([P, ends[-1]], F32, name=name, tag=name, align_bytes=MX_ALIGN)
            return [room[:, a:b] for a, b in zip(ends, ends[1:])]

        def turn_chunk0(t, prod):
            gather(prod, t, 0)
            add_turned(sums[t // 2][:, t % 2, :], [prod.rearrange("p (g j) -> p j g", j=K)[:, j, :] for j in range(K)])

        def pick_chunk3(t, picked):
            nc.scalar.activation(picked.bitcast(BF16), window(t, 3 * PIECE, PIECE), COPY)
            corners = psum.tile([P, 2, P], F32, name=f"corners{t}", tag="corners")
            pairs = picked.rearrange("p (g u) -> p u g", u=2)
            for u in range(2):
                nc.tensor.transpose(corners[:, u, :], pairs[:, u, :], ident[:])
            return corners[:].rearrange("g u p -> g (u p)").bitcast(BF16).rearrange("g (u p e) -> g u e p", u=2, e=2)

        def weigh_chunk3(t, corners):
            lead = held.tile([P, P], F32, name=f"lead{t}", tag=f"picks{t + 1}", align_bytes=MX_ALIGN)
            rest = held.tile([P, K - 1, P], F32, name=f"rest{t}", tag="rest")
            weighed = [lead[:]] + [rest[:, j, :] for j in range(K - 1)]
            for j in range(K):
                nc.scalar.activation(weighed[j], corners[:, j // 2, j % 2, :], COPY, scale=part_last[:, j : j + 1])
            add_turned(direct[t], weighed)

        def pick_half(t, picked):
            nc.scalar.activation(picked.bitcast(BF16), window(t, SPREAD - HALF, HALF), COPY)
            nc.tensor.transpose(half_turned, picked, ident[:])
            return half_turned.bitcast(BF16).rearrange("r (p e) -> r e p", e=2)

        def weigh_half(t, entries):
            weighed = held.tile([P, 2, P], F32, name=f"weighed_half{t}", tag=f"products{t + 1}", align_bytes=MX_ALIGN)
            for e in range(2):
                nc.scalar.activation(weighed[:, e, :], entries[:, e, :], COPY, scale=part_half[:, e : e + 1])
            if t % 2 == 0:
                half_sums.append(psum.tile([P, 2, P], F32, name=f"half_sums{t // 2}", tag="half_sums"))
            add_turned(half_sums[t // 2][:, t % 2, :], [weighed[:, e, :] for e in range(2)])

        def reduce_half(t0, t1):
            with nc.allow_low_precision(reason="the float32 sum is rounded to bfloat16 once"):
                nc.vector.tensor_reduce(
                    places_of(2)[:, P // 2 :, t0:t1],
                    half_sums[t0 // 2][:, t0 % 2 : t0 % 2 + t1 - t0, :].rearrange("p t (g u) -> p g t u", u=2),
                    mybir.AxisListType.X,
                    ADD,
                )

        turned = [held.tile([P, P], F32, name=f"turned{u}")[:] for u in range(2)]

        def round_sums(u, e0, e1):
            pairs = turned[u].bitcast(BF16).rearrange("g (p e) -> g p e", e=2)
            nc.scalar.copy(pairs[:, :, e0:e1], sums[u][:, e0:e1, :].rearrange("g e p -> g p e"))
            if e1 == 2:
                nc.tensor.transpose(backs[:, u, :], turned[u], ident[:])

        for t in range(PACK - 1):
            prod0, prod1, prod2 = carve(f"products{t}", [PIECE, PIECE, HALF])
            picked2, picked3 = carve(f"picks{t}", [HALF // 2, PIECE // 2])
            half_entries = pick_half(t, picked2)
            turn_chunk0(t, prod0)
            corners = pick_chunk3(t, picked3)
            if t == 0:
                part_half = picked2[:, :2]
                nc.scalar.copy(part_half, half_weights[:, :, 0])
            weigh_half(t, half_entries)
            weigh_chunk3(t, corners)
            gather(prod1, t, PIECE)
            gather(prod2, t, 2 * PIECE)
            reduce_corners(prod1, t, 1)
            reduce_corners(prod2, t, 2)
            if t == 1:
                reduce_half(0, 2)
                nc.scalar.copy(places_of(3)[:, :, 0], direct[0])
                round_sums(0, 0, 2)
        round_sums(1, 0, 1)
        reduce_half(2, 3)

        def quantize(flat, name):
            n = flat.shape[1] // PACK
            codes = held.tile([P, n], U32, name=f"codes{name}", align_bytes=MX_ALIGN)
            scales = held.tile([P, n], U8, name=f"scales{name}", align_bytes=MX_ALIGN)
            nc.vector.quantize_mx(out=codes[:].bitcast(FP8X4), scales=scales[:], in_=flat)
            return codes, scales

        def multiply(acc, h, packed):
            nc.tensor.matmul_mx(
                out=acc,
                lhsT=w_packed[0][:, h * P : (h + 1) * P].bitcast(FP8X4),
                lhsT_scale=w_packed[1][:, h * P : (h + 1) * P],
                rhs=packed[0][:].bitcast(FP8X4),
                rhs_scale=packed[1][:],
                start=True,
                stop=True,
            )

        def store(k, result):
            nc.sync.dma_start(out[:, k * P : (k + 1) * P].rearrange("(h p) g -> p h g", h=2), result[:])

        def finish_shared(k, banks, packed):
            result = held.tile([P, 2, P], F32, name=f"result{k}", align_bytes=ROW_ALIGN)
            for h, copy in enumerate((nc.scalar.copy, nc.vector.tensor_copy)):
                acc = psum.tile([P, P], F32, name=f"acc{k}{h}", tag=banks[h])
                multiply(acc[:], h, packed)
                copy(result[:, h, :], acc[:])
            store(k, result)

        t = PACK - 1
        prod0, prod12, w_room = carve(f"products{t}", [PIECE, PIECE + HALF, M * PACK // 2])
        picked2, picked3 = carve(f"picks{t}", [HALF // 2, PIECE // 2])
        w_grouped = w_room.bitcast(BF16)

        def round_w(m0, m1, copy):
            copy(
                w_grouped[:, m0 * PACK : m1 * PACK].rearrange("p (c i t) -> p c t i", i=4, t=PACK),
                w_raw[:, :, m0:m1].rearrange("p t (c i) -> p c t i", i=4),
            )

        corners = pick_chunk3(t, picked3)
        turn_chunk0(t, prod0)
        half_entries = pick_half(t, picked2)
        gather(prod12, t, PIECE)
        round_w(0, W_SPLIT, nc.vector.tensor_copy)
        round_w(W_SPLIT, M, nc.scalar.copy)
        weigh_chunk3(t, corners)
        weigh_half(t, half_entries)
        round_sums(1, 1, 2)
        nc.scalar.copy(places_of(3)[:, :, 1:], later[:].rearrange("p t g -> p g t"))
        nc.scalar.copy(grouped[0].bitcast(F32).rearrange("p (g u) -> p g u", u=2), backs[:].rearrange("p u g -> p g u"))
        reduce_corners(prod12[:, :PIECE], t, 1)
        w_packed = quantize(w_grouped, "w")

        packed1 = quantize(grouped[1], "1")
        acc = psum.tile([P, 2, P], F32, name="acc1", tag="sums01")
        for h in range(2):
            multiply(acc[:, h, :], h, packed1)
        result = held.tile([P, 2, P], F32, name="result1", align_bytes=ROW_ALIGN)
        nc.scalar.copy(result[:], acc[:])
        store(1, result)

        reduce_corners(prod12[:, PIECE:], t, 2)
        reduce_half(3, 4)
        packed = {k: quantize(grouped[k], str(k)) for k in (3, 2, 0)}
        finish_shared(3, ("shared", "later"), packed[3])
        finish_shared(2, ("corners", "spare"), packed[2])
        finish_shared(0, ("sums23", "half_sums"), packed[0])
